import numpy as np
import ml_dtypes


def mxq(x, axis, fmt="e4m3"):
    dtype, down = {"e4m3": (ml_dtypes.float8_e4m3fn, 7), "e5m2": (ml_dtypes.float8_e5m2, 14)}[fmt]
    v = np.moveaxis(np.asarray(x, np.float32).astype(ml_dtypes.bfloat16).astype(np.float64), axis, -1)
    blocks = v.reshape(v.shape[:-1] + (-1, 32))
    amax = np.abs(blocks).max(-1, keepdims=True)
    byte = np.maximum(np.where(amax > 0, np.frexp(amax)[1] - 1 + 127, 0) - down, 1)
    scale = np.exp2(byte - 127.0)
    codes = (blocks / scale).astype(np.float32).astype(dtype).astype(np.float64)
    return np.moveaxis((codes * scale).reshape(v.shape), -1, axis)


WIDE = False


def mx_kscale(k):
    if not WIDE:
        return np.ones(k)
    levels = np.array([10, -10, 5, -5, 0])
    if k % 512:
        return np.exp2(np.random.permutation(np.resize(levels, k // 32))).repeat(32)
    a = np.empty((k // 512, 16))
    for p in range(k // 512):
        a[p, :8] = np.random.permutation(np.resize(levels, 8))
        for g in range(8):
            far = levels[np.abs(levels - a[p, g]) >= 10]
            a[p, g + 8] = far[np.random.randint(len(far))]
    return np.exp2(a.ravel()).repeat(32)


def f64(x):
    return np.asarray(x).astype(np.float64)


def striped(idx):
    return np.tile(idx.reshape(-1, 16).T, (8, 1)).astype(np.uint16)


def unstriped(offs):
    return offs[:16].T.reshape(-1).astype(np.int64)


def pack_weight(w):
    k, n = w.shape
    w = f64(np.asarray(w, np.float32).astype(ml_dtypes.bfloat16)).reshape(k // 32, 32, n)
    amax = np.abs(w).max(1)
    byte = np.clip(np.where(amax > 0, np.frexp(amax)[1] - 1 + 127 - 7, 1), 1, 254)
    scaled = (w * np.exp2(127.0 - byte)[:, None, :]).reshape(k, n).astype(np.float32)
    words = np.ascontiguousarray(scaled.reshape(k // 512, 128, 4, n).transpose(0, 1, 3, 2)).astype(ml_dtypes.float8_e4m3fn).view(np.uint8)
    return words, np.ascontiguousarray(byte.astype(np.uint8).reshape(k // 512, 16, n))


def unpack_weight(words, scales):
    g, p, n, _ = words.shape
    vals = np.ascontiguousarray(words).view(ml_dtypes.float8_e4m3fn).astype(np.float64) * np.repeat(np.exp2(scales.astype(np.float64) - 127.0), 8, axis=1)[..., None]
    return vals.transpose(0, 1, 3, 2).reshape(g * 512, n)


E2M1 = np.array([0.0, 0.5, 1.0, 1.5, 2.0, 3.0, 4.0, 6.0, -0.0, -0.5, -1.0, -1.5, -2.0, -3.0, -4.0, -6.0])


def pack_fp4(w):
    k, n = w.shape
    w = f64(np.asarray(w, np.float32).astype(ml_dtypes.bfloat16)).reshape(k // 32, 32, n)
    amax = np.abs(w).max(1)
    mant, ex = np.frexp(amax / 6.0)
    byte = np.clip(np.where(amax > 0, np.where(mant > 0.5, ex, ex - 1) + 127, 1), 1, 254)
    scaled = (w * np.exp2(127.0 - byte)[:, None, :]).reshape(k, n).astype(np.float32)
    c = np.ascontiguousarray(scaled.reshape(k // 512, 128, 4, n).transpose(0, 1, 3, 2)).astype(ml_dtypes.float4_e2m1fn).view(np.uint8) & 0xF
    words = (c[..., 0::2] | (c[..., 1::2] << 4)).reshape(k // 512, 128, 2 * n)
    return np.ascontiguousarray(words), np.ascontiguousarray(byte.astype(np.uint8).reshape(k // 512, 16, n))


def unpack_fp4(words, scales):
    g, _, n = scales.shape
    words = np.ascontiguousarray(words).reshape(g, 128, n, 2)
    nib = np.empty((g, 128, n, 4), np.uint8)
    nib[..., 0::2] = words & 0xF
    nib[..., 1::2] = words >> 4
    vals = E2M1[nib] * np.repeat(np.exp2(scales.astype(np.float64) - 127.0), 8, axis=1)[..., None]
    return vals.transpose(0, 1, 3, 2).reshape(g * 512, n)


def sigmoid(v):
    return 1.0 / (1.0 + np.exp(-np.maximum(v, -700.0)))


K, T, S, H, N = 512, 1024, 512, 512, 256


def setup_inputs():
    n = np.random.standard_normal
    s = mx_kscale(K)[:, None]
    u = mx_kscale(H)
    packed_xT = pack_weight(n((K, T)) * s)
    packed_w3 = pack_fp4(n((H, N)) / np.sqrt(H) / u[:, None])
    packed_w4 = pack_fp4(n((K, N)) / np.sqrt(K) / s)
    return {
        "x_words": packed_xT[0],
        "x_scales": packed_xT[1],
        "w1": (n((K, H)) / np.sqrt(2 * K) / s * u).astype(np.float32),
        "w2": (n((K, H)) / np.sqrt(2 * K) / s * u).astype(np.float32),
        "w3_words": packed_w3[0],
        "w3_scales": packed_w3[1],
        "w4_words": packed_w4[0],
        "w4_scales": packed_w4[1],
        "offs": striped(np.random.permutation(T)[:S]),
        "dst": striped(np.random.permutation(T)[:S]),
    }


def reference(x_words, x_scales, w1, w2, w3_words, w3_scales, w4_words, w4_scales, offs, dst):
    xq = unpack_weight(x_words, x_scales)[:, unstriped(offs)]
    x_dst = unpack_weight(x_words, x_scales)[:, unstriped(dst)]
    y = mxq(f64(w1), 0, "e4m3").T @ xq + mxq(f64(w2), 0, "e4m3").T @ x_dst
    h = np.maximum(y, 0.2 * y)
    e = sigmoid(unpack_fp4(w3_words, w3_scales).T @ mxq(h, 0, "e4m3"))
    v = unpack_fp4(w4_words, w4_scales).T @ xq
    return e * v

@@ -1,0 +1,181 @@
+from contextlib import ExitStack
+
+import concourse.mybir as mybir
+
+K, T, S, H, N = 512, 1024, 512, 512, 256
+FLOPS = 2 * S * (2 * K * H + H * N + K * N)
+
+F32 = mybir.dt.float32
+BF16 = mybir.dt.bfloat16
+I32 = mybir.dt.int32
+U32 = mybir.dt.uint32
+U16 = mybir.dt.uint16
+U8 = mybir.dt.uint8
+FP8X4 = mybir.dt.float8_e4m3fn_x4
+FP4X4 = mybir.dt.float4_e2m1fn_x4
+SIGMOID = mybir.ActivationFunctionType.Sigmoid
+MULT = mybir.AluOpType.mult
+MAX = mybir.AluOpType.max
+
+P = 128
+PACK = 4
+EDGES = 128
+BLOCKS = S // EDGES
+HALVES = N // P
+CHUNK = 256
+SLOPE = 0.2
+
+
+def load_scale_rows(queue, plane, scales):
+    for q in range(4):
+        queue.dma_start(
+            out=plane[32 * q : 32 * q + 4, :].bitcast(I32),
+            in_=scales[0, 4 * q : 4 * q + 4, :].bitcast(I32),
+        )
+
+
+def tile_picked_zgatt_sigmoid_p_kernel(tc, x_words, x_scales, w1, w2, w3_words, w3_scales, w4_words, w4_scales, offs, dst, out):
+    nc = tc.nc
+    with ExitStack() as ctx:
+        keep = ctx.enter_context(tc.tile_pool(name="keep", bufs=1))
+        psum = ctx.enter_context(tc.psum_pool(name="psum", bufs=1))
+        psum_e = ctx.enter_context(tc.psum_pool(name="psum_e", bufs=2))
+
+        table_words = keep.tile([P, T], I32, align_bytes=64)
+        table_scales = keep.tile([P, T], U8, align_bytes=64)
+        src_list = keep.tile([P, S // 16], U16)
+        dst_list = keep.tile([P, S // 16], U16)
+        w3_codes = keep.tile([P, 2 * N], U8, align_bytes=64)
+        w4_codes = keep.tile([P, 2 * N], U8, align_bytes=64)
+        w3_plane = keep.tile([P, N], U8, align_bytes=64)
+        w4_plane = keep.tile([P, N], U8, align_bytes=64)
+
+        nc.vector.memset(table_scales[:].bitcast(I32), 0)
+        nc.vector.memset(w4_plane[:].bitcast(I32), 0)
+        nc.vector.memset(w3_plane[:].bitcast(I32), 0)
+
+        nc.sync.dma_start(out=table_words[:], in_=x_words[0].rearrange("p n t -> p (n t)").bitcast(I32))
+        nc.sync.dma_start(src_list[:], offs)
+        nc.sync.dma_start(dst_list[:], dst)
+        load_scale_rows(nc.gpsimd, table_scales, x_scales)
+
+        raw = {}
+        for a, w in enumerate((w1, w2)):
+            rows = w.rearrange("(p j) c -> p j c", j=PACK)
+            for c in range(H // CHUNK):
+                raw[a, c] = keep.tile([P, PACK, CHUNK], F32, name="raw_%d_%d" % (a, c))
+                nc.sync.dma_start(out=raw[a, c][:], in_=rows[:, :, c * CHUNK : (c + 1) * CHUNK])
+
+        nc.sync.dma_start(out=w4_codes[:].bitcast(I32), in_=w4_words[0].bitcast(I32))
+        load_scale_rows(nc.sync, w4_plane, w4_scales)
+        nc.sync.dma_start(out=w3_codes[:].bitcast(I32), in_=w3_words[0].bitcast(I32))
+        load_scale_rows(nc.sync, w3_plane, w3_scales)
+
+        picked = []
+        for name, offsets in (("src", src_list), ("dst", dst_list)):
+            codes = keep.tile([P, S], U32, name=name + "_codes", align_bytes=64)
+            nc.vector.tensor_copy(codes[:], table_words[:].bitcast(U32).indirect(offsets[:]))
+            picked.append(codes)
+        planes = []
+        for name, offsets in (("src", src_list), ("dst", dst_list)):
+            plane = keep.tile([P, S], U8, name=name + "_plane", align_bytes=64)
+            nc.vector.tensor_copy(plane[:], table_scales[:].indirect(offsets[:]))
+            planes.append(plane)
+
+        w_codes, w_planes = [], []
+        per_chunk = CHUNK // PACK
+        for a in range(2):
+            grouped = keep.tile([P, PACK, P, PACK], BF16, name="grouped_%d" % a, align_bytes=64)
+            for c in range(H // CHUNK):
+                to = grouped[:, :, c * per_chunk : (c + 1) * per_chunk, :].rearrange("p t m j -> p m j t")
+                frm = raw[a, c][:].rearrange("p j (m t) -> p m j t", t=PACK)
+                if (a, c) == (1, 1):
+                    nc.vector.tensor_copy(out=to, in_=frm)
+                else:
+                    nc.scalar.copy(out=to, in_=frm)
+            codes = keep.tile([P, H], U32, name="w_codes_%d" % a, align_bytes=64)
+            plane = keep.tile([P, H], U8, name="w_plane_%d" % a, align_bytes=64)
+            nc.vector.quantize_mx(
+                out=codes[:].bitcast(FP8X4),
+                scales=plane[:],
+                in_=grouped[:].rearrange("p t m j -> p (t m j)"),
+            )
+            w_codes.append(codes)
+            w_planes.append(plane)
+
+        messages = []
+        for pair in range(2):
+            bank = psum.tile([P, HALVES, 2 * EDGES], F32, name="messages_%d" % pair)
+            cols = slice(pair * 2 * EDGES, (pair + 1) * 2 * EDGES)
+            for half in range(HALVES):
+                nc.tensor.matmul_mx(
+                    out=bank[:, half, :],
+                    lhsT=w4_codes[:, 2 * P * half : 2 * P * (half + 1)].bitcast(FP4X4),
+                    lhsT_scale=w4_plane[:, P * half : P * (half + 1)],
+                    rhs=picked[0][:, cols].bitcast(FP8X4),
+                    rhs_scale=planes[0][:, cols],
+                    start=True,
+                    stop=True,
+                )
+            messages.append(bank)
+
+        out_view = out.rearrange("(h p) n -> p h n", p=P)
+
+        def first_layer(b):
+            cols = slice(b * EDGES, (b + 1) * EDGES)
+            y_bank = psum.tile([P, PACK, EDGES], F32, name="y_bank_%d" % b)
+            for t in range(PACK):
+                for a in range(2):
+                    nc.tensor.matmul_mx(
+                        out=y_bank[:, t, :],
+                        lhsT=w_codes[a][:, t * P : (t + 1) * P].bitcast(FP8X4),
+                        lhsT_scale=w_planes[a][:, t * P : (t + 1) * P],
+                        rhs=picked[a][:, cols].bitcast(FP8X4),
+                        rhs_scale=planes[a][:, cols],
+                        start=(a == 0),
+                        stop=(a == 1),
+                    )
+            y = keep.tile([P, EDGES, PACK], F32, name="y_%d" % b)
+            nc.scalar.copy(out=y[:], in_=y_bank[:].rearrange("p t n -> p n t"))
+            return y
+
+        def hidden(b, y):
+            flat = y[:].rearrange("p n t -> p (n t)")
+            h = keep.tile([P, EDGES * PACK], BF16, name="h_%d" % b, align_bytes=64)
+            nc.vector.scalar_tensor_tensor(out=h[:], in0=flat, scalar=SLOPE, in1=flat, op0=MULT, op1=MAX)
+            return h
+
+        def scores(b, h):
+            codes = keep.tile([P, EDGES], U32, name="h_codes_%d" % b, align_bytes=64)
+            plane = keep.tile([P, EDGES], U8, name="h_plane_%d" % b, align_bytes=64)
+            nc.vector.quantize_mx(out=codes[:].bitcast(FP8X4), scales=plane[:], in_=h[:])
+            bank = psum_e.tile([P, HALVES, EDGES], F32, name="score_bank")
+            for half in range(HALVES):
+                nc.tensor.matmul_mx(
+                    out=bank[:, half, :],
+                    lhsT=w3_codes[:, 2 * P * half : 2 * P * (half + 1)].bitcast(FP4X4),
+                    lhsT_scale=w3_plane[:, P * half : P * (half + 1)],
+                    rhs=codes[:].bitcast(FP8X4),
+                    rhs_scale=plane[:],
+                    start=True,
+                    stop=True,
+                )
+            e = keep.tile([P, HALVES, EDGES], F32, name="e_%d" % b)
+            nc.scalar.activation(out=e[:], in_=bank[:], func=SIGMOID)
+            return e
+
+        def weigh(b, e):
+            result = keep.tile([P, HALVES, EDGES], F32, name="result_%d" % b)
+            at = (b % 2) * EDGES
+            nc.vector.tensor_tensor(out=result[:], in0=messages[b // 2][:, :, at : at + EDGES], in1=e[:], op=MULT)
+            nc.sync.dma_start(out=out_view[:, :, b * EDGES : (b + 1) * EDGES], in_=result[:])
+
+        ys = [first_layer(b) for b in range(BLOCKS)]
+        hs, es = {}, {}
+        for step in range(BLOCKS + 2):
+            if step < BLOCKS:
+                hs[step] = hidden(step, ys[step])
+            if 1 <= step <= BLOCKS:
+                es[step - 1] = scores(step - 1, hs[step - 1])
+            if step >= 2:
+                weigh(step - 2, es[step - 2])

@@ -24,6 +24,8 @@ BLOCKS = S // EDGES
 HALVES = N // P
 CHUNK = 256
 SLOPE = 0.2
+VECTOR_SHARE = 40
+WARM_PASSES = 2
 
 
 def load_scale_rows(queue, plane, scales):
@@ -50,20 +52,24 @@ def tile_picked_zgatt_sigmoid_p_kernel(tc, x_words, x_scales, w1, w2, w3_words, 
         w3_plane = keep.tile([P, N], U8, align_bytes=64)
         w4_plane = keep.tile([P, N], U8, align_bytes=64)
 
-        nc.vector.memset(table_scales[:].bitcast(I32), 0)
-        nc.vector.memset(w4_plane[:].bitcast(I32), 0)
-        nc.vector.memset(w3_plane[:].bitcast(I32), 0)
+        nc.gpsimd.memset(table_scales[:].bitcast(I32), 0)
+        nc.gpsimd.memset(w4_plane[:].bitcast(I32), 0)
+        nc.gpsimd.memset(w3_plane[:].bitcast(I32), 0)
+        warm_in = keep.tile([P, 1], F32)
+        warm_out = keep.tile([P, 1], F32)
+        nc.vector.memset(warm_in[:], 0.0)
+        nc.scalar.activation(out=warm_out[:], in_=warm_in[:], func=SIGMOID)
 
-        nc.sync.dma_start(out=table_words[:], in_=x_words[0].rearrange("p n t -> p (n t)").bitcast(I32))
         nc.sync.dma_start(src_list[:], offs)
+        nc.sync.dma_start(out=table_words[:], in_=x_words[0].rearrange("p n t -> p (n t)").bitcast(I32))
+        load_scale_rows(nc.sync, table_scales, x_scales)
         nc.sync.dma_start(dst_list[:], dst)
-        load_scale_rows(nc.gpsimd, table_scales, x_scales)
 
         raw = {}
         for a, w in enumerate((w1, w2)):
             rows = w.rearrange("(p j) c -> p j c", j=PACK)
             for c in range(H // CHUNK):
-                raw[a, c] = keep.tile([P, PACK, CHUNK], F32, name="raw_%d_%d" % (a, c))
+                raw[a, c] = keep.tile([P, PACK, CHUNK], F32, name="raw_%d_%d" % (a, c), align_bytes=64)
                 nc.sync.dma_start(out=raw[a, c][:], in_=rows[:, :, c * CHUNK : (c + 1) * CHUNK])
 
         nc.sync.dma_start(out=w4_codes[:].bitcast(I32), in_=w4_words[0].bitcast(I32))
@@ -71,16 +77,19 @@ def tile_picked_zgatt_sigmoid_p_kernel(tc, x_words, x_scales, w1, w2, w3_words, 
         nc.sync.dma_start(out=w3_codes[:].bitcast(I32), in_=w3_words[0].bitcast(I32))
         load_scale_rows(nc.sync, w3_plane, w3_scales)
 
-        picked = []
-        for name, offsets in (("src", src_list), ("dst", dst_list)):
-            codes = keep.tile([P, S], U32, name=name + "_codes", align_bytes=64)
-            nc.vector.tensor_copy(codes[:], table_words[:].bitcast(U32).indirect(offsets[:]))
-            picked.append(codes)
-        planes = []
-        for name, offsets in (("src", src_list), ("dst", dst_list)):
-            plane = keep.tile([P, S], U8, name=name + "_plane", align_bytes=64)
-            nc.vector.tensor_copy(plane[:], table_scales[:].indirect(offsets[:]))
-            planes.append(plane)
+        words = table_words[:].bitcast(U32)
+
+        def gather(picked, table, offsets, first, count):
+            nc.vector.tensor_copy(picked, table.indirect(offsets[:, first // 16 : (first + count) // 16]))
+
+        src_codes = keep.tile([P, S], U32, align_bytes=64)
+        src_plane = keep.tile([P, S], U8, align_bytes=64)
+        dst_plane = keep.tile([P, S], U8, align_bytes=64)
+        dst_first = keep.tile([P, EDGES], U32, align_bytes=64)
+        gather(src_codes[:], words, src_list, 0, S)
+        gather(src_plane[:], table_scales[:], src_list, 0, S)
+        gather(dst_plane[:], table_scales[:], dst_list, 0, S)
+        gather(dst_first[:], words, dst_list, 0, EDGES)
 
         w_codes, w_planes = [], []
         per_chunk = CHUNK // PACK
@@ -90,39 +99,60 @@ def tile_picked_zgatt_sigmoid_p_kernel(tc, x_words, x_scales, w1, w2, w3_words, 
                 to = grouped[:, :, c * per_chunk : (c + 1) * per_chunk, :].rearrange("p t m j -> p m j t")
                 frm = raw[a, c][:].rearrange("p j (m t) -> p m j t", t=PACK)
                 if (a, c) == (1, 1):
-                    nc.vector.tensor_copy(out=to, in_=frm)
+                    nc.vector.tensor_copy(out=to[:, :VECTOR_SHARE], in_=frm[:, :VECTOR_SHARE])
+                    nc.scalar.copy(out=to[:, VECTOR_SHARE:], in_=frm[:, VECTOR_SHARE:])
                 else:
                     nc.scalar.copy(out=to, in_=frm)
             codes = keep.tile([P, H], U32, name="w_codes_%d" % a, align_bytes=64)
             plane = keep.tile([P, H], U8, name="w_plane_%d" % a, align_bytes=64)
-            nc.vector.quantize_mx(
-                out=codes[:].bitcast(FP8X4),
-                scales=plane[:],
-                in_=grouped[:].rearrange("p t m j -> p (t m j)"),
-            )
+            flat = grouped[:].rearrange("p t m j -> p (t m j)")
+            width = H if a == 0 else P
+            for c0 in range(0, H, width):
+                nc.vector.quantize_mx(
+                    out=codes[:, c0 : c0 + width].bitcast(FP8X4),
+                    scales=plane[:, c0 : c0 + width],
+                    in_=flat[:, PACK * c0 : PACK * (c0 + width)],
+                )
             w_codes.append(codes)
             w_planes.append(plane)
+            if a == 0:
+                warm_bank = psum_e.tile([P, S], F32, name="warm_bank", tag="score_bank")
+                for t in range(WARM_PASSES):
+                    nc.tensor.matmul_mx(
+                        out=warm_bank[:],
+                        lhsT=codes[:, t * P : (t + 1) * P].bitcast(FP8X4),
+                        lhsT_scale=plane[:, t * P : (t + 1) * P],
+                        rhs=src_codes[:].bitcast(FP8X4),
+                        rhs_scale=src_plane[:],
+                        start=True,
+                        stop=True,
+                    )
 
-        messages = []
-        for pair in range(2):
-            bank = psum.tile([P, HALVES, 2 * EDGES], F32, name="messages_%d" % pair)
+        dst_rest = keep.tile([P, S - EDGES], U32, tag="grouped_1", align_bytes=64)
+        gather(dst_rest[:, :EDGES], words, dst_list, EDGES, EDGES)
+        gather(dst_rest[:, EDGES:], words, dst_list, 2 * EDGES, 2 * EDGES)
+
+        def message_pair(pair):
+            bank = psum.tile([P, HALVES, 2 * EDGES], F32, name="messages_%d" % pair, tag="y_bank_%d" % pair)
             cols = slice(pair * 2 * EDGES, (pair + 1) * 2 * EDGES)
             for half in range(HALVES):
                 nc.tensor.matmul_mx(
                     out=bank[:, half, :],
                     lhsT=w4_codes[:, 2 * P * half : 2 * P * (half + 1)].bitcast(FP4X4),
                     lhsT_scale=w4_plane[:, P * half : P * (half + 1)],
-                    rhs=picked[0][:, cols].bitcast(FP8X4),
-                    rhs_scale=planes[0][:, cols],
+                    rhs=src_codes[:, cols].bitcast(FP8X4),
+                    rhs_scale=src_plane[:, cols],
                     start=True,
                     stop=True,
                 )
-            messages.append(bank)
+            return bank
 
         out_view = out.rearrange("(h p) n -> p h n", p=P)
 
         def first_layer(b):
             cols = slice(b * EDGES, (b + 1) * EDGES)
+            dst_codes = dst_first[:] if b == 0 else dst_rest[:, (b - 1) * EDGES : b * EDGES]
+            moving = ((src_codes[:, cols], src_plane[:, cols]), (dst_codes, dst_plane[:, cols]))
             y_bank = psum.tile([P, PACK, EDGES], F32, name="y_bank_%d" % b)
             for t in range(PACK):
                 for a in range(2):
@@ -130,8 +160,8 @@ def tile_picked_zgatt_sigmoid_p_kernel(tc, x_words, x_scales, w1, w2, w3_words, 
                         out=y_bank[:, t, :],
                         lhsT=w_codes[a][:, t * P : (t + 1) * P].bitcast(FP8X4),
                         lhsT_scale=w_planes[a][:, t * P : (t + 1) * P],
-                        rhs=picked[a][:, cols].bitcast(FP8X4),
-                        rhs_scale=planes[a][:, cols],
+                        rhs=moving[a][0].bitcast(FP8X4),
+                        rhs_scale=moving[a][1],
                         start=(a == 0),
                         stop=(a == 1),
                     )
@@ -170,12 +200,15 @@ def tile_picked_zgatt_sigmoid_p_kernel(tc, x_words, x_scales, w1, w2, w3_words, 
             nc.vector.tensor_tensor(out=result[:], in0=messages[b // 2][:, :, at : at + EDGES], in1=e[:], op=MULT)
             nc.sync.dma_start(out=out_view[:, :, b * EDGES : (b + 1) * EDGES], in_=result[:])
 
-        ys = [first_layer(b) for b in range(BLOCKS)]
-        hs, es = {}, {}
-        for step in range(BLOCKS + 2):
+        ys, hs, es, messages = {}, {}, {}, {}
+        for step in range(BLOCKS + 3):
+            if 2 <= step < BLOCKS + 2:
+                es[step - 2] = scores(step - 2, hs[step - 2])
+            if 1 <= step < BLOCKS + 1:
+                hs[step - 1] = hidden(step - 1, ys[step - 1])
+            if step in (2, 4):
+                messages[step // 2 - 1] = message_pair(step // 2 - 1)
+            if step >= 3:
+                weigh(step - 3, es[step - 3])
             if step < BLOCKS:
-                hs[step] = hidden(step, ys[step])
-            if 1 <= step <= BLOCKS:
-                es[step - 1] = scores(step - 1, hs[step - 1])
-            if step >= 2:
-                weigh(step - 2, es[step - 2])
+                ys[step] = first_layer(step)

@@ -24,8 +24,7 @@ BLOCKS = S // EDGES
 HALVES = N // P
 CHUNK = 256
 SLOPE = 0.2
-VECTOR_SHARE = 40
-WARM_PASSES = 2
+WARM_PASSES = 3
 
 
 def load_scale_rows(queue, plane, scales):
@@ -91,6 +90,18 @@ def tile_picked_zgatt_sigmoid_p_kernel(tc, x_words, x_scales, w1, w2, w3_words, 
         gather(dst_plane[:], table_scales[:], dst_list, 0, S)
         gather(dst_first[:], words, dst_list, 0, EDGES)
 
+        warm_bank = psum_e.tile([P, S], F32, name="warm_bank", tag="score_bank")
+        for t in range(WARM_PASSES):
+            nc.tensor.matmul_mx(
+                out=warm_bank[:],
+                lhsT=src_codes[:, :P].bitcast(FP8X4),
+                lhsT_scale=src_plane[:, :P],
+                rhs=src_codes[:].bitcast(FP8X4),
+                rhs_scale=dst_plane[:],
+                start=True,
+                stop=True,
+            )
+
         w_codes, w_planes = [], []
         per_chunk = CHUNK // PACK
         for a in range(2):
@@ -98,11 +109,11 @@ def tile_picked_zgatt_sigmoid_p_kernel(tc, x_words, x_scales, w1, w2, w3_words, 
             for c in range(H // CHUNK):
                 to = grouped[:, :, c * per_chunk : (c + 1) * per_chunk, :].rearrange("p t m j -> p m j t")
                 frm = raw[a, c][:].rearrange("p j (m t) -> p m j t", t=PACK)
-                if (a, c) == (1, 1):
-                    nc.vector.tensor_copy(out=to[:, :VECTOR_SHARE], in_=frm[:, :VECTOR_SHARE])
-                    nc.scalar.copy(out=to[:, VECTOR_SHARE:], in_=frm[:, VECTOR_SHARE:])
-                else:
-                    nc.scalar.copy(out=to, in_=frm)
+                for t0 in (0, 2):
+                    if (a, c, t0) == (1, 1, 0):
+                        nc.vector.tensor_copy(out=to[:, :, :, t0 : t0 + 2], in_=frm[:, :, :, t0 : t0 + 2])
+                    else:
+                        nc.scalar.copy(out=to[:, :, :, t0 : t0 + 2], in_=frm[:, :, :, t0 : t0 + 2])
             codes = keep.tile([P, H], U32, name="w_codes_%d" % a, align_bytes=64)
             plane = keep.tile([P, H], U8, name="w_plane_%d" % a, align_bytes=64)
             flat = grouped[:].rearrange("p t m j -> p (t m j)")
@@ -115,18 +126,6 @@ def tile_picked_zgatt_sigmoid_p_kernel(tc, x_words, x_scales, w1, w2, w3_words, 
                 )
             w_codes.append(codes)
             w_planes.append(plane)
-            if a == 0:
-                warm_bank = psum_e.tile([P, S], F32, name="warm_bank", tag="score_bank")
-                for t in range(WARM_PASSES):
-                    nc.tensor.matmul_mx(
-                        out=warm_bank[:],
-                        lhsT=codes[:, t * P : (t + 1) * P].bitcast(FP8X4),
-                        lhsT_scale=plane[:, t * P : (t + 1) * P],
-                        rhs=src_codes[:].bitcast(FP8X4),
-                        rhs_scale=src_plane[:],
-                        start=True,
-                        stop=True,
-                    )
 
         dst_rest = keep.tile([P, S - EDGES], U32, tag="grouped_1", align_bytes=64)
         gather(dst_rest[:, :EDGES], words, dst_list, EDGES, EDGES)

@@ -14,22 +14,26 @@ U8 = mybir.dt.uint8
 FP8X4 = mybir.dt.float8_e4m3fn_x4
 FP4X4 = mybir.dt.float4_e2m1fn_x4
 SIGMOID = mybir.ActivationFunctionType.Sigmoid
+COPY = mybir.ActivationFunctionType.Copy
 MULT = mybir.AluOpType.mult
 MAX = mybir.AluOpType.max
 
 P = 128
 PACK = 4
+QUADRANTS = 4
+PER_COLUMN = 16
 EDGES = 128
 BLOCKS = S // EDGES
+PAIR = 2 * EDGES
 HALVES = N // P
 CHUNK = 256
 SLOPE = 0.2
 WARM_PASSES = 3
 
 
-def load_scale_rows(queue, plane, scales):
-    for q in range(4):
-        queue.dma_start(
+def load_scale_rows(nc, plane, scales):
+    for q in range(QUADRANTS):
+        nc.sync.dma_start(
             out=plane[32 * q : 32 * q + 4, :].bitcast(I32),
             in_=scales[0, 4 * q : 4 * q + 4, :].bitcast(I32),
         )
@@ -40,20 +44,21 @@ def tile_picked_zgatt_sigmoid_p_kernel(tc, x_words, x_scales, w1, w2, w3_words, 
     with ExitStack() as ctx:
         keep = ctx.enter_context(tc.tile_pool(name="keep", bufs=1))
         psum = ctx.enter_context(tc.psum_pool(name="psum", bufs=1))
-        psum_e = ctx.enter_context(tc.psum_pool(name="psum_e", bufs=2))
+        psum_scores = ctx.enter_context(tc.psum_pool(name="psum_scores", bufs=2))
 
         table_words = keep.tile([P, T], I32, align_bytes=64)
         table_scales = keep.tile([P, T], U8, align_bytes=64)
-        src_list = keep.tile([P, S // 16], U16)
-        dst_list = keep.tile([P, S // 16], U16)
+        src_list = keep.tile([P, S // PER_COLUMN], U16)
+        dst_list = keep.tile([P, S // PER_COLUMN], U16)
         w3_codes = keep.tile([P, 2 * N], U8, align_bytes=64)
         w4_codes = keep.tile([P, 2 * N], U8, align_bytes=64)
         w3_plane = keep.tile([P, N], U8, align_bytes=64)
         w4_plane = keep.tile([P, N], U8, align_bytes=64)
 
-        nc.gpsimd.memset(table_scales[:].bitcast(I32), 0)
+        nc.vector.memset(table_scales[:].bitcast(I32), 0)
         nc.gpsimd.memset(w4_plane[:].bitcast(I32), 0)
         nc.gpsimd.memset(w3_plane[:].bitcast(I32), 0)
+
         warm_in = keep.tile([P, 1], F32)
         warm_out = keep.tile([P, 1], F32)
         nc.vector.memset(warm_in[:], 0.0)
@@ -61,43 +66,43 @@ def tile_picked_zgatt_sigmoid_p_kernel(tc, x_words, x_scales, w1, w2, w3_words, 
 
         nc.sync.dma_start(src_list[:], offs)
         nc.sync.dma_start(out=table_words[:], in_=x_words[0].rearrange("p n t -> p (n t)").bitcast(I32))
-        load_scale_rows(nc.sync, table_scales, x_scales)
         nc.sync.dma_start(dst_list[:], dst)
-
         raw = {}
         for a, w in enumerate((w1, w2)):
             rows = w.rearrange("(p j) c -> p j c", j=PACK)
             for c in range(H // CHUNK):
                 raw[a, c] = keep.tile([P, PACK, CHUNK], F32, name="raw_%d_%d" % (a, c), align_bytes=64)
                 nc.sync.dma_start(out=raw[a, c][:], in_=rows[:, :, c * CHUNK : (c + 1) * CHUNK])
-
+                if (a, c) == (0, 0):
+                    load_scale_rows(nc, table_scales, x_scales)
         nc.sync.dma_start(out=w4_codes[:].bitcast(I32), in_=w4_words[0].bitcast(I32))
-        load_scale_rows(nc.sync, w4_plane, w4_scales)
+        load_scale_rows(nc, w4_plane, w4_scales)
         nc.sync.dma_start(out=w3_codes[:].bitcast(I32), in_=w3_words[0].bitcast(I32))
-        load_scale_rows(nc.sync, w3_plane, w3_scales)
+        load_scale_rows(nc, w3_plane, w3_scales)
 
         words = table_words[:].bitcast(U32)
 
         def gather(picked, table, offsets, first, count):
-            nc.vector.tensor_copy(picked, table.indirect(offsets[:, first // 16 : (first + count) // 16]))
+            cut = offsets[:, first // PER_COLUMN : (first + count) // PER_COLUMN]
+            nc.vector.tensor_copy(picked, table.indirect(cut))
 
         src_codes = keep.tile([P, S], U32, align_bytes=64)
         src_plane = keep.tile([P, S], U8, align_bytes=64)
         dst_plane = keep.tile([P, S], U8, align_bytes=64)
         dst_first = keep.tile([P, EDGES], U32, align_bytes=64)
         gather(src_codes[:], words, src_list, 0, S)
+        gather(dst_first[:], words, dst_list, 0, EDGES)
         gather(src_plane[:], table_scales[:], src_list, 0, S)
         gather(dst_plane[:], table_scales[:], dst_list, 0, S)
-        gather(dst_first[:], words, dst_list, 0, EDGES)
 
-        warm_bank = psum_e.tile([P, S], F32, name="warm_bank", tag="score_bank")
-        for t in range(WARM_PASSES):
+        warm_bank = psum_scores.tile([P, S], F32, name="warm_bank", tag="score_bank")
+        for warm_pass in range(WARM_PASSES):
             nc.tensor.matmul_mx(
                 out=warm_bank[:],
                 lhsT=src_codes[:, :P].bitcast(FP8X4),
                 lhsT_scale=src_plane[:, :P],
                 rhs=src_codes[:].bitcast(FP8X4),
-                rhs_scale=dst_plane[:],
+                rhs_scale=src_plane[:],
                 start=True,
                 stop=True,
             )
@@ -110,7 +115,7 @@ def tile_picked_zgatt_sigmoid_p_kernel(tc, x_words, x_scales, w1, w2, w3_words, 
                 to = grouped[:, :, c * per_chunk : (c + 1) * per_chunk, :].rearrange("p t m j -> p m j t")
                 frm = raw[a, c][:].rearrange("p j (m t) -> p m j t", t=PACK)
                 for t0 in (0, 2):
-                    if (a, c, t0) == (1, 1, 0):
+                    if (a, c, t0) == (1, H // CHUNK - 1, 0):
                         nc.vector.tensor_copy(out=to[:, :, :, t0 : t0 + 2], in_=frm[:, :, :, t0 : t0 + 2])
                     else:
                         nc.scalar.copy(out=to[:, :, :, t0 : t0 + 2], in_=frm[:, :, :, t0 : t0 + 2])
@@ -129,24 +134,7 @@ def tile_picked_zgatt_sigmoid_p_kernel(tc, x_words, x_scales, w1, w2, w3_words, 
 
         dst_rest = keep.tile([P, S - EDGES], U32, tag="grouped_1", align_bytes=64)
         gather(dst_rest[:, :EDGES], words, dst_list, EDGES, EDGES)
-        gather(dst_rest[:, EDGES:], words, dst_list, 2 * EDGES, 2 * EDGES)
-
-        def message_pair(pair):
-            bank = psum.tile([P, HALVES, 2 * EDGES], F32, name="messages_%d" % pair, tag="y_bank_%d" % pair)
-            cols = slice(pair * 2 * EDGES, (pair + 1) * 2 * EDGES)
-            for half in range(HALVES):
-                nc.tensor.matmul_mx(
-                    out=bank[:, half, :],
-                    lhsT=w4_codes[:, 2 * P * half : 2 * P * (half + 1)].bitcast(FP4X4),
-                    lhsT_scale=w4_plane[:, P * half : P * (half + 1)],
-                    rhs=src_codes[:, cols].bitcast(FP8X4),
-                    rhs_scale=src_plane[:, cols],
-                    start=True,
-                    stop=True,
-                )
-            return bank
-
-        out_view = out.rearrange("(h p) n -> p h n", p=P)
+        gather(dst_rest[:, EDGES:], words, dst_list, PAIR, PAIR)
 
         def first_layer(b):
             cols = slice(b * EDGES, (b + 1) * EDGES)
@@ -164,50 +152,71 @@ def tile_picked_zgatt_sigmoid_p_kernel(tc, x_words, x_scales, w1, w2, w3_words, 
                         start=(a == 0),
                         stop=(a == 1),
                     )
-            y = keep.tile([P, EDGES, PACK], F32, name="y_%d" % b)
-            nc.scalar.copy(out=y[:], in_=y_bank[:].rearrange("p t n -> p n t"))
-            return y
+            woven = y_bank[:].rearrange("p t n -> p n t")
+            if b < BLOCKS - 1:
+                y = keep.tile([P, EDGES, PACK], F32, name="y_%d" % b)
+                nc.scalar.copy(out=y[:], in_=woven)
+                return y, None
+            y = keep.tile([P, EDGES, PACK], BF16, name="y_%d" % b)
+            sloped = keep.tile([P, EDGES, PACK], BF16)
+            nc.scalar.copy(out=y[:], in_=woven)
+            nc.scalar.activation(out=sloped[:], in_=woven, func=COPY, scale=SLOPE)
+            return y, sloped
 
-        def hidden(b, y):
-            flat = y[:].rearrange("p n t -> p (n t)")
+        def hidden(b, y, sloped):
+            y_flat = y[:].rearrange("p n t -> p (n t)")
             h = keep.tile([P, EDGES * PACK], BF16, name="h_%d" % b, align_bytes=64)
-            nc.vector.scalar_tensor_tensor(out=h[:], in0=flat, scalar=SLOPE, in1=flat, op0=MULT, op1=MAX)
+            if sloped is None:
+                nc.vector.scalar_tensor_tensor(out=h[:], in0=y_flat, scalar=SLOPE, in1=y_flat, op0=MULT, op1=MAX)
+            else:
+                nc.vector.tensor_tensor(out=h[:], in0=y_flat, in1=sloped[:].rearrange("p n t -> p (n t)"), op=MAX)
             return h
 
         def scores(b, h):
-            codes = keep.tile([P, EDGES], U32, name="h_codes_%d" % b, align_bytes=64)
-            plane = keep.tile([P, EDGES], U8, name="h_plane_%d" % b, align_bytes=64)
-            nc.vector.quantize_mx(out=codes[:].bitcast(FP8X4), scales=plane[:], in_=h[:])
-            bank = psum_e.tile([P, HALVES, EDGES], F32, name="score_bank")
+            h_codes = keep.tile([P, EDGES], U32, name="h_codes_%d" % b, align_bytes=64)
+            h_plane = keep.tile([P, EDGES], U8, name="h_plane_%d" % b, align_bytes=64)
+            nc.vector.quantize_mx(out=h_codes[:].bitcast(FP8X4), scales=h_plane[:], in_=h[:])
+            score_bank = psum_scores.tile([P, HALVES, EDGES], F32)
             for half in range(HALVES):
                 nc.tensor.matmul_mx(
-                    out=bank[:, half, :],
+                    out=score_bank[:, half, :],
                     lhsT=w3_codes[:, 2 * P * half : 2 * P * (half + 1)].bitcast(FP4X4),
                     lhsT_scale=w3_plane[:, P * half : P * (half + 1)],
-                    rhs=codes[:].bitcast(FP8X4),
-                    rhs_scale=plane[:],
+                    rhs=h_codes[:].bitcast(FP8X4),
+                    rhs_scale=h_plane[:],
                     start=True,
                     stop=True,
                 )
             e = keep.tile([P, HALVES, EDGES], F32, name="e_%d" % b)
-            nc.scalar.activation(out=e[:], in_=bank[:], func=SIGMOID)
+            nc.scalar.activation(out=e[:], in_=score_bank[:], func=SIGMOID)
             return e
 
-        def weigh(b, e):
-            result = keep.tile([P, HALVES, EDGES], F32, name="result_%d" % b)
-            at = (b % 2) * EDGES
-            nc.vector.tensor_tensor(out=result[:], in0=messages[b // 2][:, :, at : at + EDGES], in1=e[:], op=MULT)
-            nc.sync.dma_start(out=out_view[:, :, b * EDGES : (b + 1) * EDGES], in_=result[:])
+        def message_pair(pair):
+            bank = psum.tile([P, HALVES, PAIR], F32, name="messages_%d" % pair, tag="y_bank_%d" % pair)
+            cols = slice(pair * PAIR, (pair + 1) * PAIR)
+            for half in range(HALVES):
+                nc.tensor.matmul_mx(
+                    out=bank[:, half, :],
+                    lhsT=w4_codes[:, 2 * P * half : 2 * P * (half + 1)].bitcast(FP4X4),
+                    lhsT_scale=w4_plane[:, P * half : P * (half + 1)],
+                    rhs=src_codes[:, cols].bitcast(FP8X4),
+                    rhs_scale=src_plane[:, cols],
+                    start=True,
+                    stop=True,
+                )
+            return bank
 
-        ys, hs, es, messages = {}, {}, {}, {}
-        for step in range(BLOCKS + 3):
-            if 2 <= step < BLOCKS + 2:
-                es[step - 2] = scores(step - 2, hs[step - 2])
-            if 1 <= step < BLOCKS + 1:
-                hs[step - 1] = hidden(step - 1, ys[step - 1])
-            if step in (2, 4):
-                messages[step // 2 - 1] = message_pair(step // 2 - 1)
-            if step >= 3:
-                weigh(step - 3, es[step - 3])
-            if step < BLOCKS:
-                ys[step] = first_layer(step)
+        ys = [first_layer(b) for b in range(BLOCKS)]
+        es = [scores(b, hidden(b, *ys[b])) for b in range(BLOCKS)]
+        messages = [message_pair(pair) for pair in range(BLOCKS // 2)]
+        results = [keep.tile([P, HALVES, PAIR], F32, name="result_%d" % pair) for pair in range(BLOCKS // 2)]
+        out_view = out.rearrange("(half p) n -> p half n", p=P)
+
+        for b in range(BLOCKS):
+            pair = b // 2
+            within = slice((b % 2) * EDGES, (b % 2 + 1) * EDGES)
+            nc.vector.tensor_tensor(out=results[pair][:, :, within], in0=messages[pair][:, :, within], in1=es[b][:], op=MULT)
+            if b == 1:
+                nc.sync.dma_start(out=out_view[:, :, :PAIR], in_=results[pair][:])
+            elif b > 1:
+                nc.sync.dma_start(out=out_view[:, :, b * EDGES : (b + 1) * EDGES], in_=results[pair][:, :, within])

@@ -88,70 +88,100 @@ def tile_picked_zgatt_sigmoid_p_kernel(tc, x_words, x_scales, w1, w2, w3_words, 
 
         src_codes = keep.tile([P, S], U32, align_bytes=64)
         src_plane = keep.tile([P, S], U8, align_bytes=64)
-        dst_plane = keep.tile([P, S], U8, align_bytes=64)
-        dst_first = keep.tile([P, EDGES], U32, align_bytes=64)
+        dst_plane = keep.tile([P, S - EDGES], U8, align_bytes=64)
+        dst_first = keep.tile([P, PAIR], U32, align_bytes=64)
         gather(src_codes[:], words, src_list, 0, S)
-        gather(dst_first[:], words, dst_list, 0, EDGES)
+        gather(dst_first[:], words, dst_list, 0, PAIR)
         gather(src_plane[:], table_scales[:], src_list, 0, S)
-        gather(dst_plane[:], table_scales[:], dst_list, 0, S)
+        gather(dst_plane[:], table_scales[:], dst_list, 0, S - EDGES)
 
         warm_bank = psum_scores.tile([P, S], F32, name="warm_bank", tag="score_bank")
         for warm_pass in range(WARM_PASSES):
             nc.tensor.matmul_mx(
                 out=warm_bank[:],
                 lhsT=src_codes[:, :P].bitcast(FP8X4),
-                lhsT_scale=src_plane[:, :P],
+                lhsT_scale=(src_plane if warm_pass < WARM_PASSES - 1 else dst_plane)[:, :P],
                 rhs=src_codes[:].bitcast(FP8X4),
                 rhs_scale=src_plane[:],
                 start=True,
                 stop=True,
             )
 
+        def message_pair(pair):
+            bank = psum.tile([P, HALVES, PAIR], F32, name="messages_%d" % pair)
+            cols = slice(pair * PAIR, (pair + 1) * PAIR)
+            for half in range(HALVES):
+                nc.tensor.matmul_mx(
+                    out=bank[:, half, :],
+                    lhsT=w4_codes[:, 2 * P * half : 2 * P * (half + 1)].bitcast(FP4X4),
+                    lhsT_scale=w4_plane[:, P * half : P * (half + 1)],
+                    rhs=src_codes[:, cols].bitcast(FP8X4),
+                    rhs_scale=src_plane[:, cols],
+                    start=True,
+                    stop=True,
+                )
+            return bank
+
+        messages = [message_pair(pair) for pair in range(BLOCKS // 2)]
+
         w_codes, w_planes = [], []
         per_chunk = CHUNK // PACK
         for a in range(2):
-            grouped = keep.tile([P, PACK, P, PACK], BF16, name="grouped_%d" % a, align_bytes=64)
+            grouped = [keep.tile([P, 2, P, PACK], BF16, name="grouped_%d_%d" % (a, t0), align_bytes=64) for t0 in (0, 2)]
             for c in range(H // CHUNK):
-                to = grouped[:, :, c * per_chunk : (c + 1) * per_chunk, :].rearrange("p t m j -> p m j t")
                 frm = raw[a, c][:].rearrange("p j (m t) -> p m j t", t=PACK)
                 for t0 in (0, 2):
+                    to = grouped[t0 // 2][:, :, c * per_chunk : (c + 1) * per_chunk, :].rearrange("p t m j -> p m j t")
                     if (a, c, t0) == (1, H // CHUNK - 1, 0):
-                        nc.vector.tensor_copy(out=to[:, :, :, t0 : t0 + 2], in_=frm[:, :, :, t0 : t0 + 2])
+                        nc.vector.tensor_copy(out=to, in_=frm[:, :, :, t0 : t0 + 2])
                     else:
-                        nc.scalar.copy(out=to[:, :, :, t0 : t0 + 2], in_=frm[:, :, :, t0 : t0 + 2])
+                        nc.scalar.copy(out=to, in_=frm[:, :, :, t0 : t0 + 2])
             codes = keep.tile([P, H], U32, name="w_codes_%d" % a, align_bytes=64)
             plane = keep.tile([P, H], U8, name="w_plane_%d" % a, align_bytes=64)
-            flat = grouped[:].rearrange("p t m j -> p (t m j)")
-            width = H if a == 0 else P
+            width = 2 * P if a == 0 else P
             for c0 in range(0, H, width):
+                flat = grouped[c0 // (2 * P)][:].rearrange("p t m j -> p (t m j)")
+                f0 = c0 % (2 * P)
                 nc.vector.quantize_mx(
                     out=codes[:, c0 : c0 + width].bitcast(FP8X4),
                     scales=plane[:, c0 : c0 + width],
-                    in_=flat[:, PACK * c0 : PACK * (c0 + width)],
+                    in_=flat[:, PACK * f0 : PACK * (f0 + width)],
                 )
             w_codes.append(codes)
             w_planes.append(plane)
 
-        dst_rest = keep.tile([P, S - EDGES], U32, tag="grouped_1", align_bytes=64)
-        gather(dst_rest[:, :EDGES], words, dst_list, EDGES, EDGES)
-        gather(dst_rest[:, EDGES:], words, dst_list, PAIR, PAIR)
+        dst_third = keep.tile([P, EDGES], U32, tag="grouped_1_0", align_bytes=64)
+        dst_last = keep.tile([P, EDGES], U32, tag="grouped_1_2", align_bytes=64)
+        plane_last = keep.tile([P, EDGES], U8, tag="raw_1_1", align_bytes=64)
+        gather(dst_third[:], words, dst_list, PAIR, EDGES)
+        gather(plane_last[:], table_scales[:], dst_list, PAIR + EDGES, EDGES)
+        gather(dst_last[:], words, dst_list, PAIR + EDGES, EDGES)
+        dst_planes = (dst_plane[:, :EDGES], dst_plane[:, EDGES:PAIR], dst_plane[:, PAIR:], plane_last[:])
+        y_banks = [psum.tile([P, PACK, EDGES], F32, name="y_bank_%d" % b) for b in range(BLOCKS)]
+
+        def first_pass(b, t, a):
+            cols = slice(b * EDGES, (b + 1) * EDGES)
+            dst_codes = (dst_first[:, :EDGES], dst_first[:, EDGES:], dst_third[:], dst_last[:])[b]
+            moving = ((src_codes[:, cols], src_plane[:, cols]), (dst_codes, dst_planes[b]))
+            nc.tensor.matmul_mx(
+                out=y_banks[b][:, t, :],
+                lhsT=w_codes[a][:, t * P : (t + 1) * P].bitcast(FP8X4),
+                lhsT_scale=w_planes[a][:, t * P : (t + 1) * P],
+                rhs=moving[a][0].bitcast(FP8X4),
+                rhs_scale=moving[a][1],
+                start=(a == 0),
+                stop=(a == 1),
+            )
+
+        for b in range(BLOCKS):
+            first_pass(b, 0, 0)
 
         def first_layer(b):
-            cols = slice(b * EDGES, (b + 1) * EDGES)
-            dst_codes = dst_first[:] if b == 0 else dst_rest[:, (b - 1) * EDGES : b * EDGES]
-            moving = ((src_codes[:, cols], src_plane[:, cols]), (dst_codes, dst_plane[:, cols]))
-            y_bank = psum.tile([P, PACK, EDGES], F32, name="y_bank_%d" % b)
+            y_bank = y_banks[b]
             for t in range(PACK):
                 for a in range(2):
-                    nc.tensor.matmul_mx(
-                        out=y_bank[:, t, :],
-                        lhsT=w_codes[a][:, t * P : (t + 1) * P].bitcast(FP8X4),
-                        lhsT_scale=w_planes[a][:, t * P : (t + 1) * P],
-                        rhs=moving[a][0].bitcast(FP8X4),
-                        rhs_scale=moving[a][1],
-                        start=(a == 0),
-                        stop=(a == 1),
-                    )
+                    if (t, a) != (0, 0):
+                        first_pass(b, t, a)
             woven = y_bank[:].rearrange("p t n -> p n t")
             if b < BLOCKS - 1:
                 y = keep.tile([P, EDGES, PACK], F32, name="y_%d" % b)
@@ -188,34 +218,31 @@ def tile_picked_zgatt_sigmoid_p_kernel(tc, x_words, x_scales, w1, w2, w3_words, 
                     stop=True,
                 )
             e = keep.tile([P, HALVES, EDGES], F32, name="e_%d" % b)
-            nc.scalar.activation(out=e[:], in_=score_bank[:], func=SIGMOID)
+            if b < BLOCKS - 1:
+                nc.scalar.activation(out=e[:], in_=score_bank[:], func=SIGMOID)
+            else:
+                for half in range(HALVES):
+                    nc.scalar.activation(out=e[:, half, :], in_=score_bank[:, half, :], func=SIGMOID)
             return e
 
-        def message_pair(pair):
-            bank = psum.tile([P, HALVES, PAIR], F32, name="messages_%d" % pair, tag="y_bank_%d" % pair)
-            cols = slice(pair * PAIR, (pair + 1) * PAIR)
-            for half in range(HALVES):
-                nc.tensor.matmul_mx(
-                    out=bank[:, half, :],
-                    lhsT=w4_codes[:, 2 * P * half : 2 * P * (half + 1)].bitcast(FP4X4),
-                    lhsT_scale=w4_plane[:, P * half : P * (half + 1)],
-                    rhs=src_codes[:, cols].bitcast(FP8X4),
-                    rhs_scale=src_plane[:, cols],
-                    start=True,
-                    stop=True,
-                )
-            return bank
-
         ys = [first_layer(b) for b in range(BLOCKS)]
-        es = [scores(b, hidden(b, *ys[b])) for b in range(BLOCKS)]
-        messages = [message_pair(pair) for pair in range(BLOCKS // 2)]
+        hs = [hidden(0, *ys[0])]
+        es = []
+        for b in range(BLOCKS):
+            if b + 1 < BLOCKS:
+                hs.append(hidden(b + 1, *ys[b + 1]))
+            es.append(scores(b, hs[b]))
         results = [keep.tile([P, HALVES, PAIR], F32, name="result_%d" % pair) for pair in range(BLOCKS // 2)]
         out_view = out.rearrange("(half p) n -> p half n", p=P)
 
         for b in range(BLOCKS):
             pair = b // 2
             within = slice((b % 2) * EDGES, (b % 2 + 1) * EDGES)
-            nc.vector.tensor_tensor(out=results[pair][:, :, within], in0=messages[pair][:, :, within], in1=es[b][:], op=MULT)
+            if b < BLOCKS - 1:
+                nc.vector.tensor_tensor(out=results[pair][:, :, within], in0=messages[pair][:, :, within], in1=es[b][:], op=MULT)
+            else:
+                for half in range(HALVES):
+                    nc.vector.tensor_tensor(out=results[pair][:, half, within], in0=messages[pair][:, half, within], in1=es[b][:, half, :], op=MULT)
             if b == 1:
                 nc.sync.dma_start(out=out_view[:, :, :PAIR], in_=results[pair][:])
             elif b > 1:

@@ -189,8 +189,9 @@ def tile_picked_zgatt_sigmoid_p_kernel(tc, x_words, x_scales, w1, w2, w3_words, 
                 return y, None
             y = keep.tile([P, EDGES, PACK], BF16, name="y_%d" % b)
             sloped = keep.tile([P, EDGES, PACK], BF16)
-            nc.scalar.copy(out=y[:], in_=woven)
-            nc.scalar.activation(out=sloped[:], in_=woven, func=COPY, scale=SLOPE)
+            for part in (slice(0, EDGES // 2), slice(EDGES // 2, EDGES)):
+                nc.scalar.copy(out=y[:, part, :], in_=woven[:, part, :])
+                nc.scalar.activation(out=sloped[:, part, :], in_=woven[:, part, :], func=COPY, scale=SLOPE)
             return y, sloped
 
         def hidden(b, y, sloped):
@@ -199,14 +200,22 @@ def tile_picked_zgatt_sigmoid_p_kernel(tc, x_words, x_scales, w1, w2, w3_words, 
             if sloped is None:
                 nc.vector.scalar_tensor_tensor(out=h[:], in0=y_flat, scalar=SLOPE, in1=y_flat, op0=MULT, op1=MAX)
             else:
-                nc.vector.tensor_tensor(out=h[:], in0=y_flat, in1=sloped[:].rearrange("p n t -> p (n t)"), op=MAX)
+                sloped_flat = sloped[:].rearrange("p n t -> p (n t)")
+                for part in (slice(0, 2 * EDGES), slice(2 * EDGES, 4 * EDGES)):
+                    nc.vector.tensor_tensor(out=h[:, part], in0=y_flat[:, part], in1=sloped_flat[:, part], op=MAX)
             return h
 
         def scores(b, h):
             h_codes = keep.tile([P, EDGES], U32, name="h_codes_%d" % b, align_bytes=64)
             h_plane = keep.tile([P, EDGES], U8, name="h_plane_%d" % b, align_bytes=64)
-            nc.vector.quantize_mx(out=h_codes[:].bitcast(FP8X4), scales=h_plane[:], in_=h[:])
-            score_bank = psum_scores.tile([P, HALVES, EDGES], F32)
+            parts = 1 if b < BLOCKS - 1 else 2
+            for part in range(parts):
+                c0, c1 = part * EDGES // parts, (part + 1) * EDGES // parts
+                nc.vector.quantize_mx(out=h_codes[:, c0:c1].bitcast(FP8X4), scales=h_plane[:, c0:c1], in_=h[:, PACK * c0 : PACK * c1])
+            if b < 2:
+                score_bank = psum_scores.tile([P, HALVES, EDGES], F32)
+            else:
+                score_bank = psum.tile([P, HALVES, EDGES], F32, name="late_scores_%d" % b, tag="y_bank_%d" % (b - 2))
             for half in range(HALVES):
                 nc.tensor.matmul_mx(
                     out=score_bank[:, half, :],

@@ -28,14 +28,15 @@ PAIR = 2 * EDGES
 HALVES = N // P
 CHUNK = 256
 SLOPE = 0.2
-WARM_PASSES = 3
+WARM_WIDTHS = (PAIR, PAIR, PAIR, PAIR)
+ROWS = 4
 
 
 def load_scale_rows(nc, plane, scales):
     for q in range(QUADRANTS):
         nc.sync.dma_start(
-            out=plane[32 * q : 32 * q + 4, :].bitcast(I32),
-            in_=scales[0, 4 * q : 4 * q + 4, :].bitcast(I32),
+            out=plane[32 * q : 32 * q + ROWS, :].bitcast(I32),
+            in_=scales[0, ROWS * q : ROWS * (q + 1), :].bitcast(I32),
         )
 
 
@@ -43,8 +44,8 @@ def tile_picked_zgatt_sigmoid_p_kernel(tc, x_words, x_scales, w1, w2, w3_words, 
     nc = tc.nc
     with ExitStack() as ctx:
         keep = ctx.enter_context(tc.tile_pool(name="keep", bufs=1))
+        last = ctx.enter_context(tc.tile_pool(name="last", bufs=1))
         psum = ctx.enter_context(tc.psum_pool(name="psum", bufs=1))
-        psum_scores = ctx.enter_context(tc.psum_pool(name="psum_scores", bufs=2))
 
         table_words = keep.tile([P, T], I32, align_bytes=64)
         table_scales = keep.tile([P, T], U8, align_bytes=64)
@@ -54,31 +55,40 @@ def tile_picked_zgatt_sigmoid_p_kernel(tc, x_words, x_scales, w1, w2, w3_words, 
         w4_codes = keep.tile([P, 2 * N], U8, align_bytes=64)
         w3_plane = keep.tile([P, N], U8, align_bytes=64)
         w4_plane = keep.tile([P, N], U8, align_bytes=64)
+        chunks = H // CHUNK
+        raw = {}
+        for a in range(2):
+            for c in range(chunks):
+                if (a, c) == (1, chunks - 1):
+                    raw[a, c] = last.tile([P, PACK, CHUNK], F32, name="raw_last", align_bytes=64, offset=0)
+                else:
+                    raw[a, c] = keep.tile([P, PACK, CHUNK], F32, name="raw_%d_%d" % (a, c), align_bytes=64)
+
+        def load_chunk(queue, a, c):
+            rows = (w1, w2)[a].rearrange("(p j) c -> p j c", j=PACK)
+            queue.dma_start(out=raw[a, c][:], in_=rows[:, :, c * CHUNK : (c + 1) * CHUNK])
 
         nc.vector.memset(table_scales[:].bitcast(I32), 0)
-        nc.gpsimd.memset(w4_plane[:].bitcast(I32), 0)
+        nc.sync.dma_start(out=table_words[:], in_=x_words[0].rearrange("p n t -> p (n t)").bitcast(I32))
+        nc.sync.dma_start(src_list[:], offs)
+        nc.sync.dma_start(dst_list[:], dst)
+        load_chunk(nc.sync, 0, 0)
+        load_scale_rows(nc, table_scales, x_scales)
+        load_chunk(nc.sync, 0, 1)
+        load_chunk(nc.sync, 1, 0)
+        load_chunk(nc.sync, 1, 1)
+
         nc.gpsimd.memset(w3_plane[:].bitcast(I32), 0)
+        nc.gpsimd.memset(w4_plane[:].bitcast(I32), 0)
+        nc.sync.dma_start(out=w4_codes[:].bitcast(I32), in_=w4_words[0].bitcast(I32))
+        load_scale_rows(nc, w4_plane, w4_scales)
+        nc.sync.dma_start(out=w3_codes[:].bitcast(I32), in_=w3_words[0].bitcast(I32))
+        load_scale_rows(nc, w3_plane, w3_scales)
 
         warm_in = keep.tile([P, 1], F32)
         warm_out = keep.tile([P, 1], F32)
         nc.vector.memset(warm_in[:], 0.0)
         nc.scalar.activation(out=warm_out[:], in_=warm_in[:], func=SIGMOID)
-
-        nc.sync.dma_start(src_list[:], offs)
-        nc.sync.dma_start(out=table_words[:], in_=x_words[0].rearrange("p n t -> p (n t)").bitcast(I32))
-        nc.sync.dma_start(dst_list[:], dst)
-        raw = {}
-        for a, w in enumerate((w1, w2)):
-            rows = w.rearrange("(p j) c -> p j c", j=PACK)
-            for c in range(H // CHUNK):
-                raw[a, c] = keep.tile([P, PACK, CHUNK], F32, name="raw_%d_%d" % (a, c), align_bytes=64)
-                nc.sync.dma_start(out=raw[a, c][:], in_=rows[:, :, c * CHUNK : (c + 1) * CHUNK])
-                if (a, c) == (0, 0):
-                    load_scale_rows(nc, table_scales, x_scales)
-        nc.sync.dma_start(out=w4_codes[:].bitcast(I32), in_=w4_words[0].bitcast(I32))
-        load_scale_rows(nc, w4_plane, w4_scales)
-        nc.sync.dma_start(out=w3_codes[:].bitcast(I32), in_=w3_words[0].bitcast(I32))
-        load_scale_rows(nc, w3_plane, w3_scales)
 
         words = table_words[:].bitcast(U32)
 
@@ -86,103 +96,98 @@ def tile_picked_zgatt_sigmoid_p_kernel(tc, x_words, x_scales, w1, w2, w3_words, 
             cut = offsets[:, first // PER_COLUMN : (first + count) // PER_COLUMN]
             nc.vector.tensor_copy(picked, table.indirect(cut))
 
-        src_codes = keep.tile([P, S], U32, align_bytes=64)
+        src_first = keep.tile([P, S - EDGES], U32, align_bytes=64)
         src_plane = keep.tile([P, S], U8, align_bytes=64)
         dst_plane = keep.tile([P, S - EDGES], U8, align_bytes=64)
         dst_first = keep.tile([P, PAIR], U32, align_bytes=64)
-        gather(src_codes[:], words, src_list, 0, S)
+        gather(src_first[:], words, src_list, 0, S - EDGES)
         gather(dst_first[:], words, dst_list, 0, PAIR)
-        gather(src_plane[:], table_scales[:], src_list, 0, S)
+        for first in (0, PAIR):
+            gather(src_plane[:, first : first + PAIR], table_scales[:], src_list, first, PAIR)
         gather(dst_plane[:], table_scales[:], dst_list, 0, S - EDGES)
 
-        warm_bank = psum_scores.tile([P, S], F32, name="warm_bank", tag="score_bank")
-        for warm_pass in range(WARM_PASSES):
+        warm_bank = psum.tile([P, S], F32, name="warm_bank", tag="score_bank_0")
+        for width in WARM_WIDTHS:
             nc.tensor.matmul_mx(
-                out=warm_bank[:],
-                lhsT=src_codes[:, :P].bitcast(FP8X4),
-                lhsT_scale=(src_plane if warm_pass < WARM_PASSES - 1 else dst_plane)[:, :P],
-                rhs=src_codes[:].bitcast(FP8X4),
-                rhs_scale=src_plane[:],
+                out=warm_bank[:, :width],
+                lhsT=src_first[:, :P].bitcast(FP8X4),
+                lhsT_scale=src_plane[:, :P],
+                rhs=src_first[:, :width].bitcast(FP8X4),
+                rhs_scale=src_plane[:, :width],
                 start=True,
                 stop=True,
             )
 
-        def message_pair(pair):
-            bank = psum.tile([P, HALVES, PAIR], F32, name="messages_%d" % pair)
-            cols = slice(pair * PAIR, (pair + 1) * PAIR)
-            for half in range(HALVES):
-                nc.tensor.matmul_mx(
-                    out=bank[:, half, :],
-                    lhsT=w4_codes[:, 2 * P * half : 2 * P * (half + 1)].bitcast(FP4X4),
-                    lhsT_scale=w4_plane[:, P * half : P * (half + 1)],
-                    rhs=src_codes[:, cols].bitcast(FP8X4),
-                    rhs_scale=src_plane[:, cols],
-                    start=True,
-                    stop=True,
-                )
-            return bank
-
-        messages = [message_pair(pair) for pair in range(BLOCKS // 2)]
-
-        w_codes, w_planes = [], []
         per_chunk = CHUNK // PACK
-        for a in range(2):
-            grouped = [keep.tile([P, 2, P, PACK], BF16, name="grouped_%d_%d" % (a, t0), align_bytes=64) for t0 in (0, 2)]
-            for c in range(H // CHUNK):
-                frm = raw[a, c][:].rearrange("p j (m t) -> p m j t", t=PACK)
-                for t0 in (0, 2):
-                    to = grouped[t0 // 2][:, :, c * per_chunk : (c + 1) * per_chunk, :].rearrange("p t m j -> p m j t")
-                    if (a, c, t0) == (1, H // CHUNK - 1, 0):
-                        nc.vector.tensor_copy(out=to, in_=frm[:, :, :, t0 : t0 + 2])
-                    else:
-                        nc.scalar.copy(out=to, in_=frm[:, :, :, t0 : t0 + 2])
-            codes = keep.tile([P, H], U32, name="w_codes_%d" % a, align_bytes=64)
-            plane = keep.tile([P, H], U8, name="w_plane_%d" % a, align_bytes=64)
-            width = 2 * P if a == 0 else P
-            for c0 in range(0, H, width):
-                flat = grouped[c0 // (2 * P)][:].rearrange("p t m j -> p (t m j)")
-                f0 = c0 % (2 * P)
-                nc.vector.quantize_mx(
-                    out=codes[:, c0 : c0 + width].bitcast(FP8X4),
-                    scales=plane[:, c0 : c0 + width],
-                    in_=flat[:, PACK * f0 : PACK * (f0 + width)],
-                )
-            w_codes.append(codes)
-            w_planes.append(plane)
+        w_codes = [keep.tile([P, PACK, P], U32, name="w_codes_%d" % a, align_bytes=64) for a in range(2)]
+        w_planes = [keep.tile([P, PACK, P], U8, name="w_plane_%d" % a, align_bytes=64) for a in range(2)]
 
-        dst_third = keep.tile([P, EDGES], U32, tag="grouped_1_0", align_bytes=64)
-        dst_last = keep.tile([P, EDGES], U32, tag="grouped_1_2", align_bytes=64)
-        plane_last = keep.tile([P, EDGES], U8, tag="raw_1_1", align_bytes=64)
-        gather(dst_third[:], words, dst_list, PAIR, EDGES)
-        gather(plane_last[:], table_scales[:], dst_list, PAIR + EDGES, EDGES)
-        gather(dst_last[:], words, dst_list, PAIR + EDGES, EDGES)
-        dst_planes = (dst_plane[:, :EDGES], dst_plane[:, EDGES:PAIR], dst_plane[:, PAIR:], plane_last[:])
-        y_banks = [psum.tile([P, PACK, EDGES], F32, name="y_bank_%d" % b) for b in range(BLOCKS)]
+        def cast(copy, to, a, c, t0):
+            frm = raw[a, c][:].rearrange("p j (m t) -> p m j t", t=PACK)
+            copy(out=to.rearrange("p t m j -> p m j t"), in_=frm[:, :, :, t0 : t0 + 2])
 
-        def first_pass(b, t, a):
-            cols = slice(b * EDGES, (b + 1) * EDGES)
-            dst_codes = (dst_first[:, :EDGES], dst_first[:, EDGES:], dst_third[:], dst_last[:])[b]
-            moving = ((src_codes[:, cols], src_plane[:, cols]), (dst_codes, dst_planes[b]))
-            nc.tensor.matmul_mx(
-                out=y_banks[b][:, t, :],
-                lhsT=w_codes[a][:, t * P : (t + 1) * P].bitcast(FP8X4),
-                lhsT_scale=w_planes[a][:, t * P : (t + 1) * P],
-                rhs=moving[a][0].bitcast(FP8X4),
-                rhs_scale=moving[a][1],
-                start=(a == 0),
-                stop=(a == 1),
+        grouped_w1 = [keep.tile([P, 2, P, PACK], BF16, name="grouped_w1_%d" % t0, align_bytes=64) for t0 in (0, 2)]
+        for c in range(chunks):
+            for t0 in (0, 2):
+                cast(nc.scalar.copy, grouped_w1[t0 // 2][:, :, c * per_chunk : (c + 1) * per_chunk, :], 0, c, t0)
+        for t0 in (0, 2):
+            nc.vector.quantize_mx(
+                out=w_codes[0][:, t0 : t0 + 2, :].rearrange("p t m -> p (t m)").bitcast(FP8X4),
+                scales=w_planes[0][:, t0 : t0 + 2, :].rearrange("p t m -> p (t m)"),
+                in_=grouped_w1[t0 // 2][:].rearrange("p t m j -> p (t m j)"),
             )
 
-        for b in range(BLOCKS):
-            first_pass(b, 0, 0)
+        plane_last = keep.tile([P, EDGES], U8, tag="raw_1_0", align_bytes=64)
+        gather(plane_last[:], table_scales[:], dst_list, S - EDGES, EDGES)
+
+        y_banks = [psum.tile([P, PACK, EDGES], F32, name="y_bank_%d" % b) for b in range(BLOCKS)]
+
+        def first_pass(b, t, a, codes, plane):
+            nc.tensor.matmul_mx(
+                out=y_banks[b][:, t, :],
+                lhsT=w_codes[a][:, t, :].bitcast(FP8X4),
+                lhsT_scale=w_planes[a][:, t, :],
+                rhs=codes.bitcast(FP8X4),
+                rhs_scale=plane,
+                start=(a == 0 and t == 0),
+                stop=(a == 1 and t == PACK - 1),
+            )
+
+        for t0 in (0, 2):
+            for b in range(BLOCKS - 1):
+                cols = slice(b * EDGES, (b + 1) * EDGES)
+                for t in (t0, t0 + 1):
+                    first_pass(b, t, 0, src_first[:, cols], src_plane[:, cols])
+
+        grouped_w2 = [keep.tile([P, 2, P, PACK], BF16, name="grouped_w2_%d" % t0, align_bytes=64) for t0 in (0, 2)]
+        for c in range(chunks):
+            for t0 in (0, 2):
+                copy = nc.vector.tensor_copy if (c, t0) == (chunks - 1, 0) else nc.scalar.copy
+                cast(copy, grouped_w2[t0 // 2][:, :, c * per_chunk : (c + 1) * per_chunk, :], 1, c, t0)
+        for t in range(PACK):
+            nc.vector.quantize_mx(
+                out=w_codes[1][:, t, :].bitcast(FP8X4),
+                scales=w_planes[1][:, t, :],
+                in_=grouped_w2[t // 2][:, t % 2, :, :].rearrange("p m j -> p (m j)"),
+            )
+
+        dst_third = last.tile([P, EDGES], U32, align_bytes=64, offset=0)
+        src_last = last.tile([P, EDGES], U32, align_bytes=64, offset=4 * EDGES)
+        dst_last = last.tile([P, EDGES], U32, align_bytes=64, offset=8 * EDGES)
+        gather(dst_third[:], words, dst_list, PAIR, EDGES)
+        gather(src_last[:], words, src_list, S - EDGES, EDGES)
+        gather(dst_last[:], words, dst_list, S - EDGES, EDGES)
+        src_codes = (src_first[:, :EDGES], src_first[:, EDGES:PAIR], src_first[:, PAIR:], src_last[:])
+        dst_codes = (dst_first[:, :EDGES], dst_first[:, EDGES:], dst_third[:], dst_last[:])
+        dst_planes = (dst_plane[:, :EDGES], dst_plane[:, EDGES:PAIR], dst_plane[:, PAIR:], plane_last[:])
 
         def first_layer(b):
-            y_bank = y_banks[b]
+            if b == BLOCKS - 1:
+                for t in range(PACK):
+                    first_pass(b, t, 0, src_last[:], src_plane[:, S - EDGES :])
             for t in range(PACK):
-                for a in range(2):
-                    if (t, a) != (0, 0):
-                        first_pass(b, t, a)
-            woven = y_bank[:].rearrange("p t n -> p n t")
+                first_pass(b, t, 1, dst_codes[b], dst_planes[b])
+            woven = y_banks[b][:].rearrange("p t n -> p n t")
             if b < BLOCKS - 1:
                 y = keep.tile([P, EDGES, PACK], F32, name="y_%d" % b)
                 nc.scalar.copy(out=y[:], in_=woven)
@@ -193,6 +198,25 @@ def tile_picked_zgatt_sigmoid_p_kernel(tc, x_words, x_scales, w1, w2, w3_words, 
                 nc.scalar.copy(out=y[:, part, :], in_=woven[:, part, :])
                 nc.scalar.activation(out=sloped[:, part, :], in_=woven[:, part, :], func=COPY, scale=SLOPE)
             return y, sloped
+
+        def message_pair(pair):
+            bank = psum.tile([P, HALVES, PAIR], F32, name="messages_%d" % pair, tag="y_bank_%d" % pair)
+            if pair == 0:
+                pieces = [(src_first[:, :PAIR], 0, PAIR)]
+            else:
+                pieces = [(src_codes[b], b * EDGES, EDGES) for b in (2, 3)]
+            for codes, first, count in pieces:
+                for half in range(HALVES):
+                    nc.tensor.matmul_mx(
+                        out=bank[:, half, first % PAIR : first % PAIR + count],
+                        lhsT=w4_codes[:, 2 * P * half : 2 * P * (half + 1)].bitcast(FP4X4),
+                        lhsT_scale=w4_plane[:, P * half : P * (half + 1)],
+                        rhs=codes.bitcast(FP8X4),
+                        rhs_scale=src_plane[:, first : first + count],
+                        start=True,
+                        stop=True,
+                    )
+            return bank
 
         def hidden(b, y, sloped):
             y_flat = y[:].rearrange("p n t -> p (n t)")
@@ -212,10 +236,7 @@ def tile_picked_zgatt_sigmoid_p_kernel(tc, x_words, x_scales, w1, w2, w3_words, 
             for part in range(parts):
                 c0, c1 = part * EDGES // parts, (part + 1) * EDGES // parts
                 nc.vector.quantize_mx(out=h_codes[:, c0:c1].bitcast(FP8X4), scales=h_plane[:, c0:c1], in_=h[:, PACK * c0 : PACK * c1])
-            if b < 2:
-                score_bank = psum_scores.tile([P, HALVES, EDGES], F32)
-            else:
-                score_bank = psum.tile([P, HALVES, EDGES], F32, name="late_scores_%d" % b, tag="y_bank_%d" % (b - 2))
+            score_bank = psum.tile([P, HALVES, EDGES], F32, name="score_bank_%d" % b)
             for half in range(HALVES):
                 nc.tensor.matmul_mx(
                     out=score_bank[:, half, :],
@@ -235,6 +256,7 @@ def tile_picked_zgatt_sigmoid_p_kernel(tc, x_words, x_scales, w1, w2, w3_words, 
             return e
 
         ys = [first_layer(b) for b in range(BLOCKS)]
+        messages = [message_pair(pair) for pair in range(BLOCKS // 2)]
         hs = [hidden(0, *ys[0])]
         es = []
         for b in range(BLOCKS):

@@ -137,8 +137,6 @@ def tile_picked_zgatt_sigmoid_p_kernel(tc, x_words, x_scales, w1, w2, w3_words, 
                 in_=grouped_w1[t0 // 2][:].rearrange("p t m j -> p (t m j)"),
             )
 
-        plane_last = keep.tile([P, EDGES], U8, tag="raw_1_0", align_bytes=64)
-        gather(plane_last[:], table_scales[:], dst_list, S - EDGES, EDGES)
 
         y_banks = [psum.tile([P, PACK, EDGES], F32, name="y_bank_%d" % b) for b in range(BLOCKS)]
 
@@ -159,24 +157,28 @@ def tile_picked_zgatt_sigmoid_p_kernel(tc, x_words, x_scales, w1, w2, w3_words, 
                 for t in (t0, t0 + 1):
                     first_pass(b, t, 0, src_first[:, cols], src_plane[:, cols])
 
-        grouped_w2 = [keep.tile([P, 2, P, PACK], BF16, name="grouped_w2_%d" % t0, align_bytes=64) for t0 in (0, 2)]
         for c in range(chunks):
-            for t0 in (0, 2):
-                copy = nc.vector.tensor_copy if (c, t0) == (chunks - 1, 0) else nc.scalar.copy
-                cast(copy, grouped_w2[t0 // 2][:, :, c * per_chunk : (c + 1) * per_chunk, :], 1, c, t0)
-        for t in range(PACK):
-            nc.vector.quantize_mx(
-                out=w_codes[1][:, t, :].bitcast(FP8X4),
-                scales=w_planes[1][:, t, :],
-                in_=grouped_w2[t // 2][:, t % 2, :, :].rearrange("p m j -> p (m j)"),
-            )
+            grouped = []
+            for t0, copy in ((0, nc.vector.tensor_copy), (2, nc.scalar.copy)):
+                pair = keep.tile([P, 2, per_chunk, PACK], BF16, name="grouped_w2_%d_%d" % (c, t0), align_bytes=64)
+                cast(copy, pair[:], 1, c, t0)
+                grouped.append(pair)
+            within = slice(c * per_chunk, (c + 1) * per_chunk)
+            for t in range(PACK):
+                nc.vector.quantize_mx(
+                    out=w_codes[1][:, t, within].bitcast(FP8X4),
+                    scales=w_planes[1][:, t, within],
+                    in_=grouped[t // 2][:, t % 2, :, :].rearrange("p m j -> p (m j)"),
+                )
 
         dst_third = last.tile([P, EDGES], U32, align_bytes=64, offset=0)
         src_last = last.tile([P, EDGES], U32, align_bytes=64, offset=4 * EDGES)
         dst_last = last.tile([P, EDGES], U32, align_bytes=64, offset=8 * EDGES)
+        plane_last = last.tile([P, EDGES], U8, align_bytes=64, offset=12 * EDGES)
         gather(dst_third[:], words, dst_list, PAIR, EDGES)
         gather(src_last[:], words, src_list, S - EDGES, EDGES)
         gather(dst_last[:], words, dst_list, S - EDGES, EDGES)
+        gather(plane_last[:], table_scales[:], dst_list, S - EDGES, EDGES)
         src_codes = (src_first[:, :EDGES], src_first[:, EDGES:PAIR], src_first[:, PAIR:], src_last[:])
         dst_codes = (dst_first[:, :EDGES], dst_first[:, EDGES:], dst_third[:], dst_last[:])
         dst_planes = (dst_plane[:, :EDGES], dst_plane[:, EDGES:PAIR], dst_plane[:, PAIR:], plane_last[:])

@@ -239,9 +239,12 @@ def tile_picked_zgatt_sigmoid_p_kernel(tc, x_words, x_scales, w1, w2, w3_words, 
                 c0, c1 = part * EDGES // parts, (part + 1) * EDGES // parts
                 nc.vector.quantize_mx(out=h_codes[:, c0:c1].bitcast(FP8X4), scales=h_plane[:, c0:c1], in_=h[:, PACK * c0 : PACK * c1])
             score_bank = psum.tile([P, HALVES, EDGES], F32, name="score_bank_%d" % b)
+            sums = [score_bank[:, half, :] for half in range(HALVES)]
+            if b == BLOCKS - 1:
+                sums[1] = psum.tile([P, EDGES], F32, name="last_scores", tag="y_bank_2")[:]
             for half in range(HALVES):
                 nc.tensor.matmul_mx(
-                    out=score_bank[:, half, :],
+                    out=sums[half],
                     lhsT=w3_codes[:, 2 * P * half : 2 * P * (half + 1)].bitcast(FP4X4),
                     lhsT_scale=w3_plane[:, P * half : P * (half + 1)],
                     rhs=h_codes[:].bitcast(FP8X4),
@@ -254,7 +257,7 @@ def tile_picked_zgatt_sigmoid_p_kernel(tc, x_words, x_scales, w1, w2, w3_words, 
                 nc.scalar.activation(out=e[:], in_=score_bank[:], func=SIGMOID)
             else:
                 for half in range(HALVES):
-                    nc.scalar.activation(out=e[:, half, :], in_=score_bank[:, half, :], func=SIGMOID)
+                    nc.scalar.activation(out=e[:, half, :], in_=sums[half], func=SIGMOID)
             return e
 
         ys = [first_layer(b) for b in range(BLOCKS)]
@@ -276,7 +279,6 @@ def tile_picked_zgatt_sigmoid_p_kernel(tc, x_words, x_scales, w1, w2, w3_words, 
             else:
                 for half in range(HALVES):
                     nc.vector.tensor_tensor(out=results[pair][:, half, within], in0=messages[pair][:, half, within], in1=es[b][:, half, :], op=MULT)
+                    nc.sync.dma_start(out=out_view[:, half, PAIR:], in_=results[pair][:, half, :])
             if b == 1:
                 nc.sync.dma_start(out=out_view[:, :, :PAIR], in_=results[pair][:])
-            elif b > 1:
-                nc.sync.dma_start(out=out_view[:, :, b * EDGES : (b + 1) * EDGES], in_=results[pair][:, :, within])

@@ -28,7 +28,7 @@ PAIR = 2 * EDGES
 HALVES = N // P
 CHUNK = 256
 SLOPE = 0.2
-WARM_WIDTHS = (PAIR, PAIR, PAIR, PAIR)
+WARM_WIDTHS = (PAIR, PAIR)
 ROWS = 4
 
 
@@ -96,14 +96,13 @@ def tile_picked_zgatt_sigmoid_p_kernel(tc, x_words, x_scales, w1, w2, w3_words, 
             cut = offsets[:, first // PER_COLUMN : (first + count) // PER_COLUMN]
             nc.vector.tensor_copy(picked, table.indirect(cut))
 
-        src_first = keep.tile([P, S - EDGES], U32, align_bytes=64)
-        src_plane = keep.tile([P, S], U8, align_bytes=64)
+        src_first = keep.tile([P, S], U32, align_bytes=64)
+        src_plane = keep.tile([P, PAIR], U8, align_bytes=64)
         dst_plane = keep.tile([P, S - EDGES], U8, align_bytes=64)
         dst_first = keep.tile([P, PAIR], U32, align_bytes=64)
-        gather(src_first[:], words, src_list, 0, S - EDGES)
+        gather(src_first[:], words, src_list, 0, S)
         gather(dst_first[:], words, dst_list, 0, PAIR)
-        for first in (0, PAIR):
-            gather(src_plane[:, first : first + PAIR], table_scales[:], src_list, first, PAIR)
+        gather(src_plane[:], table_scales[:], src_list, 0, PAIR)
         gather(dst_plane[:], table_scales[:], dst_list, 0, S - EDGES)
 
         warm_bank = psum.tile([P, S], F32, name="warm_bank", tag="score_bank_0")
@@ -152,7 +151,7 @@ def tile_picked_zgatt_sigmoid_p_kernel(tc, x_words, x_scales, w1, w2, w3_words, 
             )
 
         for t0 in (0, 2):
-            for b in range(BLOCKS - 1):
+            for b in range(2):
                 cols = slice(b * EDGES, (b + 1) * EDGES)
                 for t in (t0, t0 + 1):
                     first_pass(b, t, 0, src_first[:, cols], src_plane[:, cols])
@@ -171,22 +170,26 @@ def tile_picked_zgatt_sigmoid_p_kernel(tc, x_words, x_scales, w1, w2, w3_words, 
                     in_=grouped[t // 2][:, t % 2, :, :].rearrange("p m j -> p (m j)"),
                 )
 
-        dst_third = last.tile([P, EDGES], U32, align_bytes=64, offset=0)
-        src_last = last.tile([P, EDGES], U32, align_bytes=64, offset=4 * EDGES)
-        dst_last = last.tile([P, EDGES], U32, align_bytes=64, offset=8 * EDGES)
-        plane_last = last.tile([P, EDGES], U8, align_bytes=64, offset=12 * EDGES)
-        gather(dst_third[:], words, dst_list, PAIR, EDGES)
-        gather(src_last[:], words, src_list, S - EDGES, EDGES)
-        gather(dst_last[:], words, dst_list, S - EDGES, EDGES)
-        gather(plane_last[:], table_scales[:], dst_list, S - EDGES, EDGES)
-        src_codes = (src_first[:, :EDGES], src_first[:, EDGES:PAIR], src_first[:, PAIR:], src_last[:])
-        dst_codes = (dst_first[:, :EDGES], dst_first[:, EDGES:], dst_third[:], dst_last[:])
-        dst_planes = (dst_plane[:, :EDGES], dst_plane[:, EDGES:PAIR], dst_plane[:, PAIR:], plane_last[:])
+        src_codes = [src_first[:, b * EDGES : (b + 1) * EDGES] for b in range(BLOCKS)]
+        dst_codes = [dst_first[:, b * EDGES : (b + 1) * EDGES] for b in range(2)]
+        src_planes = [src_plane[:, b * EDGES : (b + 1) * EDGES] for b in range(2)]
+        dst_planes = [dst_plane[:, b * EDGES : (b + 1) * EDGES] for b in range(BLOCKS - 1)]
+        late_gathers = (
+            (src_planes, U8, table_scales[:], src_list),
+            (dst_codes, U32, words, dst_list),
+            (src_planes, U8, table_scales[:], src_list),
+            (dst_codes, U32, words, dst_list),
+            (dst_planes, U8, table_scales[:], dst_list),
+        )
+        for i, (pieces, dtype, table, offsets) in enumerate(late_gathers):
+            late = last.tile([P, EDGES], dtype, name="late_%d" % i, align_bytes=64, offset=4 * EDGES * i)
+            gather(late[:], table, offsets, len(pieces) * EDGES, EDGES)
+            pieces.append(late[:])
 
         def first_layer(b):
-            if b == BLOCKS - 1:
+            if b >= 2:
                 for t in range(PACK):
-                    first_pass(b, t, 0, src_last[:], src_plane[:, S - EDGES :])
+                    first_pass(b, t, 0, src_codes[b], src_planes[b])
             for t in range(PACK):
                 first_pass(b, t, 1, dst_codes[b], dst_planes[b])
             woven = y_banks[b][:].rearrange("p t n -> p n t")
@@ -214,7 +217,7 @@ def tile_picked_zgatt_sigmoid_p_kernel(tc, x_words, x_scales, w1, w2, w3_words, 
                         lhsT=w4_codes[:, 2 * P * half : 2 * P * (half + 1)].bitcast(FP4X4),
                         lhsT_scale=w4_plane[:, P * half : P * (half + 1)],
                         rhs=codes.bitcast(FP8X4),
-                        rhs_scale=src_plane[:, first : first + count],
+                        rhs_scale=src_plane[:] if pair == 0 else src_planes[first // EDGES],
                         start=True,
                         stop=True,
                     )

@@ -97,12 +97,12 @@ def tile_picked_zgatt_sigmoid_p_kernel(tc, x_words, x_scales, w1, w2, w3_words, 
             nc.vector.tensor_copy(picked, table.indirect(cut))
 
         src_first = keep.tile([P, S], U32, align_bytes=64)
-        src_plane = keep.tile([P, PAIR], U8, align_bytes=64)
+        src_plane = keep.tile([P, S - EDGES], U8, align_bytes=64)
         dst_plane = keep.tile([P, S - EDGES], U8, align_bytes=64)
-        dst_first = keep.tile([P, PAIR], U32, align_bytes=64)
+        dst_first = keep.tile([P, EDGES], U32, align_bytes=64)
         gather(src_first[:], words, src_list, 0, S)
-        gather(dst_first[:], words, dst_list, 0, PAIR)
-        gather(src_plane[:], table_scales[:], src_list, 0, PAIR)
+        gather(dst_first[:], words, dst_list, 0, EDGES)
+        gather(src_plane[:], table_scales[:], src_list, 0, S - EDGES)
         gather(dst_plane[:], table_scales[:], dst_list, 0, S - EDGES)
 
         warm_bank = psum.tile([P, S], F32, name="warm_bank", tag="score_bank_0")
@@ -151,7 +151,7 @@ def tile_picked_zgatt_sigmoid_p_kernel(tc, x_words, x_scales, w1, w2, w3_words, 
             )
 
         for t0 in (0, 2):
-            for b in range(2):
+            for b in range(BLOCKS - 1):
                 cols = slice(b * EDGES, (b + 1) * EDGES)
                 for t in (t0, t0 + 1):
                     first_pass(b, t, 0, src_first[:, cols], src_plane[:, cols])
@@ -171,11 +171,11 @@ def tile_picked_zgatt_sigmoid_p_kernel(tc, x_words, x_scales, w1, w2, w3_words, 
                 )
 
         src_codes = [src_first[:, b * EDGES : (b + 1) * EDGES] for b in range(BLOCKS)]
-        dst_codes = [dst_first[:, b * EDGES : (b + 1) * EDGES] for b in range(2)]
-        src_planes = [src_plane[:, b * EDGES : (b + 1) * EDGES] for b in range(2)]
+        dst_codes = [dst_first[:]]
+        src_planes = [src_plane[:, b * EDGES : (b + 1) * EDGES] for b in range(BLOCKS - 1)]
         dst_planes = [dst_plane[:, b * EDGES : (b + 1) * EDGES] for b in range(BLOCKS - 1)]
         late_gathers = (
-            (src_planes, U8, table_scales[:], src_list),
+            (dst_codes, U32, words, dst_list),
             (dst_codes, U32, words, dst_list),
             (src_planes, U8, table_scales[:], src_list),
             (dst_codes, U32, words, dst_list),
@@ -187,7 +187,7 @@ def tile_picked_zgatt_sigmoid_p_kernel(tc, x_words, x_scales, w1, w2, w3_words, 
             pieces.append(late[:])
 
         def first_layer(b):
-            if b >= 2:
+            if b == BLOCKS - 1:
                 for t in range(PACK):
                     first_pass(b, t, 0, src_codes[b], src_planes[b])
             for t in range(PACK):
@@ -217,7 +217,7 @@ def tile_picked_zgatt_sigmoid_p_kernel(tc, x_words, x_scales, w1, w2, w3_words, 
                         lhsT=w4_codes[:, 2 * P * half : 2 * P * (half + 1)].bitcast(FP4X4),
                         lhsT_scale=w4_plane[:, P * half : P * (half + 1)],
                         rhs=codes.bitcast(FP8X4),
-                        rhs_scale=src_plane[:] if pair == 0 else src_planes[first // EDGES],
+                        rhs_scale=src_plane[:, :PAIR] if pair == 0 else src_planes[first // EDGES],
                         start=True,
                         stop=True,
                     )

@@ -85,10 +85,8 @@ def tile_picked_zgatt_sigmoid_p_kernel(tc, x_words, x_scales, w1, w2, w3_words, 
         nc.sync.dma_start(out=w3_codes[:].bitcast(I32), in_=w3_words[0].bitcast(I32))
         load_scale_rows(nc, w3_plane, w3_scales)
 
-        warm_in = keep.tile([P, 1], F32)
-        warm_out = keep.tile([P, 1], F32)
-        nc.vector.memset(warm_in[:], 0.0)
-        nc.scalar.activation(out=warm_out[:], in_=warm_in[:], func=SIGMOID)
+        warm = keep.tile([P, 1], U32)
+        nc.scalar.activation(out=warm[:], in_=warm[:], func=SIGMOID, scale=0.0)
 
         words = table_words[:].bitcast(U32)
 
@@ -96,13 +94,13 @@ def tile_picked_zgatt_sigmoid_p_kernel(tc, x_words, x_scales, w1, w2, w3_words, 
             cut = offsets[:, first // PER_COLUMN : (first + count) // PER_COLUMN]
             nc.vector.tensor_copy(picked, table.indirect(cut))
 
-        src_first = keep.tile([P, S], U32, align_bytes=64)
-        src_plane = keep.tile([P, S - EDGES], U8, align_bytes=64)
+        src_first = keep.tile([P, S - EDGES], U32, align_bytes=64)
+        src_plane = keep.tile([P, S], U8, align_bytes=64)
         dst_plane = keep.tile([P, S - EDGES], U8, align_bytes=64)
         dst_first = keep.tile([P, EDGES], U32, align_bytes=64)
-        gather(src_first[:], words, src_list, 0, S)
+        gather(src_first[:], words, src_list, 0, S - EDGES)
         gather(dst_first[:], words, dst_list, 0, EDGES)
-        gather(src_plane[:], table_scales[:], src_list, 0, S - EDGES)
+        gather(src_plane[:], table_scales[:], src_list, 0, S)
         gather(dst_plane[:], table_scales[:], dst_list, 0, S - EDGES)
 
         warm_bank = psum.tile([P, S], F32, name="warm_bank", tag="score_bank_0")
@@ -170,14 +168,14 @@ def tile_picked_zgatt_sigmoid_p_kernel(tc, x_words, x_scales, w1, w2, w3_words, 
                     in_=grouped[t // 2][:, t % 2, :, :].rearrange("p m j -> p (m j)"),
                 )
 
-        src_codes = [src_first[:, b * EDGES : (b + 1) * EDGES] for b in range(BLOCKS)]
+        src_codes = [src_first[:, b * EDGES : (b + 1) * EDGES] for b in range(BLOCKS - 1)]
         dst_codes = [dst_first[:]]
-        src_planes = [src_plane[:, b * EDGES : (b + 1) * EDGES] for b in range(BLOCKS - 1)]
+        src_planes = [src_plane[:, b * EDGES : (b + 1) * EDGES] for b in range(BLOCKS)]
         dst_planes = [dst_plane[:, b * EDGES : (b + 1) * EDGES] for b in range(BLOCKS - 1)]
         late_gathers = (
             (dst_codes, U32, words, dst_list),
             (dst_codes, U32, words, dst_list),
-            (src_planes, U8, table_scales[:], src_list),
+            (src_codes, U32, words, src_list),
             (dst_codes, U32, words, dst_list),
             (dst_planes, U8, table_scales[:], dst_list),
         )

@@ -28,7 +28,6 @@ PAIR = 2 * EDGES
 HALVES = N // P
 CHUNK = 256
 SLOPE = 0.2
-WARM_WIDTHS = (PAIR, PAIR)
 ROWS = 4
 
 
@@ -68,6 +67,11 @@ def tile_picked_zgatt_sigmoid_p_kernel(tc, x_words, x_scales, w1, w2, w3_words, 
             rows = (w1, w2)[a].rearrange("(p j) c -> p j c", j=PACK)
             queue.dma_start(out=raw[a, c][:], in_=rows[:, :, c * CHUNK : (c + 1) * CHUNK])
 
+        warm = keep.tile([P, 1], F32)
+        warmed = keep.tile([P, 1], F32)
+        nc.vector.memset(warm[:], 0.0)
+        nc.scalar.activation(out=warmed[:], in_=warm[:], func=SIGMOID)
+
         nc.vector.memset(table_scales[:].bitcast(I32), 0)
         nc.sync.dma_start(out=table_words[:], in_=x_words[0].rearrange("p n t -> p (n t)").bitcast(I32))
         nc.sync.dma_start(src_list[:], offs)
@@ -85,9 +89,6 @@ def tile_picked_zgatt_sigmoid_p_kernel(tc, x_words, x_scales, w1, w2, w3_words, 
         nc.sync.dma_start(out=w3_codes[:].bitcast(I32), in_=w3_words[0].bitcast(I32))
         load_scale_rows(nc, w3_plane, w3_scales)
 
-        warm = keep.tile([P, 1], U32)
-        nc.scalar.activation(out=warm[:], in_=warm[:], func=SIGMOID, scale=0.0)
-
         words = table_words[:].bitcast(U32)
 
         def gather(picked, table, offsets, first, count):
@@ -102,18 +103,6 @@ def tile_picked_zgatt_sigmoid_p_kernel(tc, x_words, x_scales, w1, w2, w3_words, 
         gather(dst_first[:], words, dst_list, 0, EDGES)
         gather(src_plane[:], table_scales[:], src_list, 0, S)
         gather(dst_plane[:], table_scales[:], dst_list, 0, S - EDGES)
-
-        warm_bank = psum.tile([P, S], F32, name="warm_bank", tag="score_bank_0")
-        for width in WARM_WIDTHS:
-            nc.tensor.matmul_mx(
-                out=warm_bank[:, :width],
-                lhsT=src_first[:, :P].bitcast(FP8X4),
-                lhsT_scale=src_plane[:, :P],
-                rhs=src_first[:, :width].bitcast(FP8X4),
-                rhs_scale=src_plane[:, :width],
-                start=True,
-                stop=True,
-            )
 
         per_chunk = CHUNK // PACK
         w_codes = [keep.tile([P, PACK, P], U32, name="w_codes_%d" % a, align_bytes=64) for a in range(2)]

@@ -69,10 +69,9 @@ def tile_picked_zgatt_sigmoid_p_kernel(tc, x_words, x_scales, w1, w2, w3_words, 
 
         warm = keep.tile([P, 1], F32)
         warmed = keep.tile([P, 1], F32)
+        nc.vector.memset(table_scales[:].bitcast(I32), 0)
         nc.vector.memset(warm[:], 0.0)
         nc.scalar.activation(out=warmed[:], in_=warm[:], func=SIGMOID)
-
-        nc.vector.memset(table_scales[:].bitcast(I32), 0)
         nc.sync.dma_start(out=table_words[:], in_=x_words[0].rearrange("p n t -> p (n t)").bitcast(I32))
         nc.sync.dma_start(src_list[:], offs)
         nc.sync.dma_start(dst_list[:], dst)

@@ -69,8 +69,8 @@ def tile_picked_zgatt_sigmoid_p_kernel(tc, x_words, x_scales, w1, w2, w3_words, 
 
         warm = keep.tile([P, 1], F32)
         warmed = keep.tile([P, 1], F32)
-        nc.vector.memset(table_scales[:].bitcast(I32), 0)
-        nc.vector.memset(warm[:], 0.0)
+        nc.gpsimd.memset(table_scales[:].bitcast(I32), 0)
+        nc.gpsimd.memset(warm[:], 0.0)
         nc.scalar.activation(out=warmed[:], in_=warm[:], func=SIGMOID)
         nc.sync.dma_start(out=table_words[:], in_=x_words[0].rearrange("p n t -> p (n t)").bitcast(I32))
         nc.sync.dma_start(src_list[:], offs)

@@ -28,6 +28,7 @@ PAIR = 2 * EDGES
 HALVES = N // P
 CHUNK = 256
 SLOPE = 0.2
+LINE = 256
 ROWS = 4
 
 
@@ -46,22 +47,22 @@ def tile_picked_zgatt_sigmoid_p_kernel(tc, x_words, x_scales, w1, w2, w3_words, 
         last = ctx.enter_context(tc.tile_pool(name="last", bufs=1))
         psum = ctx.enter_context(tc.psum_pool(name="psum", bufs=1))
 
-        table_words = keep.tile([P, T], I32, align_bytes=64)
-        table_scales = keep.tile([P, T], U8, align_bytes=64)
-        src_list = keep.tile([P, S // PER_COLUMN], U16)
-        dst_list = keep.tile([P, S // PER_COLUMN], U16)
-        w3_codes = keep.tile([P, 2 * N], U8, align_bytes=64)
-        w4_codes = keep.tile([P, 2 * N], U8, align_bytes=64)
-        w3_plane = keep.tile([P, N], U8, align_bytes=64)
-        w4_plane = keep.tile([P, N], U8, align_bytes=64)
+        table_words = keep.tile([P, T], I32, align_bytes=LINE)
+        table_scales = keep.tile([P, T], U8, align_bytes=LINE)
+        src_list = keep.tile([P, S // PER_COLUMN], U16, align_bytes=LINE)
+        dst_list = keep.tile([P, S // PER_COLUMN], U16, align_bytes=LINE)
+        w3_codes = keep.tile([P, 2 * N], U8, align_bytes=LINE)
+        w4_codes = keep.tile([P, 2 * N], U8, align_bytes=LINE)
+        w3_plane = keep.tile([P, N], U8, align_bytes=LINE)
+        w4_plane = keep.tile([P, N], U8, align_bytes=LINE)
         chunks = H // CHUNK
         raw = {}
         for a in range(2):
             for c in range(chunks):
                 if (a, c) == (1, chunks - 1):
-                    raw[a, c] = last.tile([P, PACK, CHUNK], F32, name="raw_last", align_bytes=64, offset=0)
+                    raw[a, c] = last.tile([P, PACK, CHUNK], F32, name="raw_last", align_bytes=LINE, offset=0)
                 else:
-                    raw[a, c] = keep.tile([P, PACK, CHUNK], F32, name="raw_%d_%d" % (a, c), align_bytes=64)
+                    raw[a, c] = keep.tile([P, PACK, CHUNK], F32, name="raw_%d_%d" % (a, c), align_bytes=LINE)
 
         def load_chunk(queue, a, c):
             rows = (w1, w2)[a].rearrange("(p j) c -> p j c", j=PACK)
@@ -94,24 +95,24 @@ def tile_picked_zgatt_sigmoid_p_kernel(tc, x_words, x_scales, w1, w2, w3_words, 
             cut = offsets[:, first // PER_COLUMN : (first + count) // PER_COLUMN]
             nc.vector.tensor_copy(picked, table.indirect(cut))
 
-        src_first = keep.tile([P, S - EDGES], U32, align_bytes=64)
-        src_plane = keep.tile([P, S], U8, align_bytes=64)
-        dst_plane = keep.tile([P, S - EDGES], U8, align_bytes=64)
-        dst_first = keep.tile([P, EDGES], U32, align_bytes=64)
+        src_first = keep.tile([P, S - EDGES], U32, align_bytes=LINE)
+        src_plane = keep.tile([P, S], U8, align_bytes=LINE)
+        dst_plane = keep.tile([P, S - EDGES], U8, align_bytes=LINE)
+        dst_first = keep.tile([P, EDGES], U32, align_bytes=LINE)
         gather(src_first[:], words, src_list, 0, S - EDGES)
         gather(dst_first[:], words, dst_list, 0, EDGES)
         gather(src_plane[:], table_scales[:], src_list, 0, S)
         gather(dst_plane[:], table_scales[:], dst_list, 0, S - EDGES)
 
         per_chunk = CHUNK // PACK
-        w_codes = [keep.tile([P, PACK, P], U32, name="w_codes_%d" % a, align_bytes=64) for a in range(2)]
-        w_planes = [keep.tile([P, PACK, P], U8, name="w_plane_%d" % a, align_bytes=64) for a in range(2)]
+        w_codes = [keep.tile([P, PACK, P], U32, name="w_codes_%d" % a, align_bytes=LINE) for a in range(2)]
+        w_planes = [keep.tile([P, PACK, P], U8, name="w_plane_%d" % a, align_bytes=LINE) for a in range(2)]
 
         def cast(copy, to, a, c, t0):
             frm = raw[a, c][:].rearrange("p j (m t) -> p m j t", t=PACK)
             copy(out=to.rearrange("p t m j -> p m j t"), in_=frm[:, :, :, t0 : t0 + 2])
 
-        grouped_w1 = [keep.tile([P, 2, P, PACK], BF16, name="grouped_w1_%d" % t0, align_bytes=64) for t0 in (0, 2)]
+        grouped_w1 = [keep.tile([P, 2, P, PACK], BF16, name="grouped_w1_%d" % t0, align_bytes=LINE) for t0 in (0, 2)]
         for c in range(chunks):
             for t0 in (0, 2):
                 cast(nc.scalar.copy, grouped_w1[t0 // 2][:, :, c * per_chunk : (c + 1) * per_chunk, :], 0, c, t0)
@@ -145,7 +146,7 @@ def tile_picked_zgatt_sigmoid_p_kernel(tc, x_words, x_scales, w1, w2, w3_words, 
         for c in range(chunks):
             grouped = []
             for t0, copy in ((0, nc.vector.tensor_copy), (2, nc.scalar.copy)):
-                pair = keep.tile([P, 2, per_chunk, PACK], BF16, name="grouped_w2_%d_%d" % (c, t0), align_bytes=64)
+                pair = keep.tile([P, 2, per_chunk, PACK], BF16, name="grouped_w2_%d_%d" % (c, t0), align_bytes=LINE)
                 cast(copy, pair[:], 1, c, t0)
                 grouped.append(pair)
             within = slice(c * per_chunk, (c + 1) * per_chunk)
@@ -168,7 +169,7 @@ def tile_picked_zgatt_sigmoid_p_kernel(tc, x_words, x_scales, w1, w2, w3_words, 
             (dst_planes, U8, table_scales[:], dst_list),
         )
         for i, (pieces, dtype, table, offsets) in enumerate(late_gathers):
-            late = last.tile([P, EDGES], dtype, name="late_%d" % i, align_bytes=64, offset=4 * EDGES * i)
+            late = last.tile([P, EDGES], dtype, name="late_%d" % i, align_bytes=LINE, offset=4 * EDGES * i)
             gather(late[:], table, offsets, len(pieces) * EDGES, EDGES)
             pieces.append(late[:])
 
@@ -180,11 +181,11 @@ def tile_picked_zgatt_sigmoid_p_kernel(tc, x_words, x_scales, w1, w2, w3_words, 
                 first_pass(b, t, 1, dst_codes[b], dst_planes[b])
             woven = y_banks[b][:].rearrange("p t n -> p n t")
             if b < BLOCKS - 1:
-                y = keep.tile([P, EDGES, PACK], F32, name="y_%d" % b)
+                y = keep.tile([P, EDGES, PACK], F32, name="y_%d" % b, align_bytes=LINE)
                 nc.scalar.copy(out=y[:], in_=woven)
                 return y, None
-            y = keep.tile([P, EDGES, PACK], BF16, name="y_%d" % b)
-            sloped = keep.tile([P, EDGES, PACK], BF16)
+            y = keep.tile([P, EDGES, PACK], BF16, name="y_%d" % b, align_bytes=LINE)
+            sloped = keep.tile([P, EDGES, PACK], BF16, align_bytes=LINE)
             for part in (slice(0, EDGES // 2), slice(EDGES // 2, EDGES)):
                 nc.scalar.copy(out=y[:, part, :], in_=woven[:, part, :])
                 nc.scalar.activation(out=sloped[:, part, :], in_=woven[:, part, :], func=COPY, scale=SLOPE)
@@ -211,7 +212,7 @@ def tile_picked_zgatt_sigmoid_p_kernel(tc, x_words, x_scales, w1, w2, w3_words, 
 
         def hidden(b, y, sloped):
             y_flat = y[:].rearrange("p n t -> p (n t)")
-            h = keep.tile([P, EDGES * PACK], BF16, name="h_%d" % b, align_bytes=64)
+            h = keep.tile([P, EDGES * PACK], BF16, name="h_%d" % b, align_bytes=LINE)
             if sloped is None:
                 nc.vector.scalar_tensor_tensor(out=h[:], in0=y_flat, scalar=SLOPE, in1=y_flat, op0=MULT, op1=MAX)
             else:
@@ -221,8 +222,8 @@ def tile_picked_zgatt_sigmoid_p_kernel(tc, x_words, x_scales, w1, w2, w3_words, 
             return h
 
         def scores(b, h):
-            h_codes = keep.tile([P, EDGES], U32, name="h_codes_%d" % b, align_bytes=64)
-            h_plane = keep.tile([P, EDGES], U8, name="h_plane_%d" % b, align_bytes=64)
+            h_codes = keep.tile([P, EDGES], U32, name="h_codes_%d" % b, align_bytes=LINE)
+            h_plane = keep.tile([P, EDGES], U8, name="h_plane_%d" % b, align_bytes=LINE)
             parts = 1 if b < BLOCKS - 1 else 2
             for part in range(parts):
                 c0, c1 = part * EDGES // parts, (part + 1) * EDGES // parts
@@ -241,7 +242,7 @@ def tile_picked_zgatt_sigmoid_p_kernel(tc, x_words, x_scales, w1, w2, w3_words, 
                     start=True,
                     stop=True,
                 )
-            e = keep.tile([P, HALVES, EDGES], F32, name="e_%d" % b)
+            e = keep.tile([P, HALVES, EDGES], F32, name="e_%d" % b, align_bytes=LINE)
             if b < BLOCKS - 1:
                 nc.scalar.activation(out=e[:], in_=score_bank[:], func=SIGMOID)
             else:
@@ -257,7 +258,7 @@ def tile_picked_zgatt_sigmoid_p_kernel(tc, x_words, x_scales, w1, w2, w3_words, 
             if b + 1 < BLOCKS:
                 hs.append(hidden(b + 1, *ys[b + 1]))
             es.append(scores(b, hs[b]))
-        results = [keep.tile([P, HALVES, PAIR], F32, name="result_%d" % pair) for pair in range(BLOCKS // 2)]
+        results = [keep.tile([P, HALVES, PAIR], F32, name="result_%d" % pair, align_bytes=LINE) for pair in range(BLOCKS // 2)]
         out_view = out.rearrange("(half p) n -> p half n", p=P)
 
         for b in range(BLOCKS):

from contextlib import ExitStack

import concourse.mybir as mybir

K, T, S, H, N = 512, 1024, 512, 512, 256
FLOPS = 2 * S * (2 * K * H + H * N + K * N)

F32 = mybir.dt.float32
BF16 = mybir.dt.bfloat16
I32 = mybir.dt.int32
U32 = mybir.dt.uint32
U16 = mybir.dt.uint16
U8 = mybir.dt.uint8
FP8X4 = mybir.dt.float8_e4m3fn_x4
FP4X4 = mybir.dt.float4_e2m1fn_x4
SIGMOID = mybir.ActivationFunctionType.Sigmoid
COPY = mybir.ActivationFunctionType.Copy
MULT = mybir.AluOpType.mult
MAX = mybir.AluOpType.max

P = 128
PACK = 4
QUADRANTS = 4
PER_COLUMN = 16
EDGES = 128
BLOCKS = S // EDGES
PAIR = 2 * EDGES
HALVES = N // P
CHUNK = 256
SLOPE = 0.2
LINE = 256
ROWS = 4


def load_scale_rows(nc, plane, scales):
    for q in range(QUADRANTS):
        nc.sync.dma_start(
            out=plane[32 * q : 32 * q + ROWS, :].bitcast(I32),
            in_=scales[0, ROWS * q : ROWS * (q + 1), :].bitcast(I32),
        )


def tile_picked_zgatt_sigmoid_p_kernel(tc, x_words, x_scales, w1, w2, w3_words, w3_scales, w4_words, w4_scales, offs, dst, out):
    nc = tc.nc
    with ExitStack() as ctx:
        keep = ctx.enter_context(tc.tile_pool(name="keep", bufs=1))
        last = ctx.enter_context(tc.tile_pool(name="last", bufs=1))
        psum = ctx.enter_context(tc.psum_pool(name="psum", bufs=1))

        table_words = keep.tile([P, T], I32, align_bytes=LINE)
        table_scales = keep.tile([P, T], U8, align_bytes=LINE)
        src_list = keep.tile([P, S // PER_COLUMN], U16, align_bytes=LINE)
        dst_list = keep.tile([P, S // PER_COLUMN], U16, align_bytes=LINE)
        w3_codes = keep.tile([P, 2 * N], U8, align_bytes=LINE)
        w4_codes = keep.tile([P, 2 * N], U8, align_bytes=LINE)
        w3_plane = keep.tile([P, N], U8, align_bytes=LINE)
        w4_plane = keep.tile([P, N], U8, align_bytes=LINE)
        chunks = H // CHUNK
        raw = {}
        for a in range(2):
            for c in range(chunks):
                if (a, c) == (1, chunks - 1):
                    raw[a, c] = last.tile([P, PACK, CHUNK], F32, name="raw_last", align_bytes=LINE, offset=0)
                else:
                    raw[a, c] = keep.tile([P, PACK, CHUNK], F32, name="raw_%d_%d" % (a, c), align_bytes=LINE)

        def load_chunk(queue, a, c):
            rows = (w1, w2)[a].rearrange("(p j) c -> p j c", j=PACK)
            queue.dma_start(out=raw[a, c][:], in_=rows[:, :, c * CHUNK : (c + 1) * CHUNK])

        warm = keep.tile([P, 1], F32)
        warmed = keep.tile([P, 1], F32)
        nc.gpsimd.memset(table_scales[:].bitcast(I32), 0)
        nc.gpsimd.memset(warm[:], 0.0)
        nc.scalar.activation(out=warmed[:], in_=warm[:], func=SIGMOID)
        nc.sync.dma_start(out=table_words[:], in_=x_words[0].rearrange("p n t -> p (n t)").bitcast(I32))
        nc.sync.dma_start(src_list[:], offs)
        nc.sync.dma_start(dst_list[:], dst)
        load_chunk(nc.sync, 0, 0)
        load_scale_rows(nc, table_scales, x_scales)
        load_chunk(nc.sync, 0, 1)
        load_chunk(nc.sync, 1, 0)
        load_chunk(nc.sync, 1, 1)

        nc.gpsimd.memset(w3_plane[:].bitcast(I32), 0)
        nc.gpsimd.memset(w4_plane[:].bitcast(I32), 0)
        nc.sync.dma_start(out=w4_codes[:].bitcast(I32), in_=w4_words[0].bitcast(I32))
        load_scale_rows(nc, w4_plane, w4_scales)
        nc.sync.dma_start(out=w3_codes[:].bitcast(I32), in_=w3_words[0].bitcast(I32))
        load_scale_rows(nc, w3_plane, w3_scales)

        words = table_words[:].bitcast(U32)

        def gather(picked, table, offsets, first, count):
            cut = offsets[:, first // PER_COLUMN : (first + count) // PER_COLUMN]
            nc.vector.tensor_copy(picked, table.indirect(cut))

        src_first = keep.tile([P, S - EDGES], U32, align_bytes=LINE)
        src_plane = keep.tile([P, S], U8, align_bytes=LINE)
        dst_plane = keep.tile([P, S - EDGES], U8, align_bytes=LINE)
        dst_first = keep.tile([P, EDGES], U32, align_bytes=LINE)
        gather(src_first[:], words, src_list, 0, S - EDGES)
        gather(dst_first[:], words, dst_list, 0, EDGES)
        gather(src_plane[:], table_scales[:], src_list, 0, S)
        gather(dst_plane[:], table_scales[:], dst_list, 0, S - EDGES)

        per_chunk = CHUNK // PACK
        w_codes = [keep.tile([P, PACK, P], U32, name="w_codes_%d" % a, align_bytes=LINE) for a in range(2)]
        w_planes = [keep.tile([P, PACK, P], U8, name="w_plane_%d" % a, align_bytes=LINE) for a in range(2)]

        def cast(copy, to, a, c, t0):
            frm = raw[a, c][:].rearrange("p j (m t) -> p m j t", t=PACK)
            copy(out=to.rearrange("p t m j -> p m j t"), in_=frm[:, :, :, t0 : t0 + 2])

        grouped_w1 = [keep.tile([P, 2, P, PACK], BF16, name="grouped_w1_%d" % t0, align_bytes=LINE) for t0 in (0, 2)]
        for c in range(chunks):
            for t0 in (0, 2):
                cast(nc.scalar.copy, grouped_w1[t0 // 2][:, :, c * per_chunk : (c + 1) * per_chunk, :], 0, c, t0)
        for t0 in (0, 2):
            nc.vector.quantize_mx(
                out=w_codes[0][:, t0 : t0 + 2, :].rearrange("p t m -> p (t m)").bitcast(FP8X4),
                scales=w_planes[0][:, t0 : t0 + 2, :].rearrange("p t m -> p (t m)"),
                in_=grouped_w1[t0 // 2][:].rearrange("p t m j -> p (t m j)"),
            )


        y_banks = [psum.tile([P, PACK, EDGES], F32, name="y_bank_%d" % b) for b in range(BLOCKS)]

        def first_pass(b, t, a, codes, plane):
            nc.tensor.matmul_mx(
                out=y_banks[b][:, t, :],
                lhsT=w_codes[a][:, t, :].bitcast(FP8X4),
                lhsT_scale=w_planes[a][:, t, :],
                rhs=codes.bitcast(FP8X4),
                rhs_scale=plane,
                start=(a == 0 and t == 0),
                stop=(a == 1 and t == PACK - 1),
            )

        for t0 in (0, 2):
            for b in range(BLOCKS - 1):
                cols = slice(b * EDGES, (b + 1) * EDGES)
                for t in (t0, t0 + 1):
                    first_pass(b, t, 0, src_first[:, cols], src_plane[:, cols])

        for c in range(chunks):
            grouped = []
            for t0, copy in ((0, nc.vector.tensor_copy), (2, nc.scalar.copy)):
                pair = keep.tile([P, 2, per_chunk, PACK], BF16, name="grouped_w2_%d_%d" % (c, t0), align_bytes=LINE)
                cast(copy, pair[:], 1, c, t0)
                grouped.append(pair)
            within = slice(c * per_chunk, (c + 1) * per_chunk)
            for t in range(PACK):
                nc.vector.quantize_mx(
                    out=w_codes[1][:, t, within].bitcast(FP8X4),
                    scales=w_planes[1][:, t, within],
                    in_=grouped[t // 2][:, t % 2, :, :].rearrange("p m j -> p (m j)"),
                )

        src_codes = [src_first[:, b * EDGES : (b + 1) * EDGES] for b in range(BLOCKS - 1)]
        dst_codes = [dst_first[:]]
        src_planes = [src_plane[:, b * EDGES : (b + 1) * EDGES] for b in range(BLOCKS)]
        dst_planes = [dst_plane[:, b * EDGES : (b + 1) * EDGES] for b in range(BLOCKS - 1)]
        late_gathers = (
            (dst_codes, U32, words, dst_list),
            (dst_codes, U32, words, dst_list),
            (src_codes, U32, words, src_list),
            (dst_codes, U32, words, dst_list),
            (dst_planes, U8, table_scales[:], dst_list),
        )
        for i, (pieces, dtype, table, offsets) in enumerate(late_gathers):
            late = last.tile([P, EDGES], dtype, name="late_%d" % i, align_bytes=LINE, offset=4 * EDGES * i)
            gather(late[:], table, offsets, len(pieces) * EDGES, EDGES)
            pieces.append(late[:])

        def first_layer(b):
            if b == BLOCKS - 1:
                for t in range(PACK):
                    first_pass(b, t, 0, src_codes[b], src_planes[b])
            for t in range(PACK):
                first_pass(b, t, 1, dst_codes[b], dst_planes[b])
            woven = y_banks[b][:].rearrange("p t n -> p n t")
            if b < BLOCKS - 1:
                y = keep.tile([P, EDGES, PACK], F32, name="y_%d" % b, align_bytes=LINE)
                nc.scalar.copy(out=y[:], in_=woven)
                return y, None
            y = keep.tile([P, EDGES, PACK], BF16, name="y_%d" % b, align_bytes=LINE)
            sloped = keep.tile([P, EDGES, PACK], BF16, align_bytes=LINE)
            for part in (slice(0, EDGES // 2), slice(EDGES // 2, EDGES)):
                nc.scalar.copy(out=y[:, part, :], in_=woven[:, part, :])
                nc.scalar.activation(out=sloped[:, part, :], in_=woven[:, part, :], func=COPY, scale=SLOPE)
            return y, sloped

        def message_pair(pair):
            bank = psum.tile([P, HALVES, PAIR], F32, name="messages_%d" % pair, tag="y_bank_%d" % pair)
            if pair == 0:
                pieces = [(src_first[:, :PAIR], 0, PAIR)]
            else:
                pieces = [(src_codes[b], b * EDGES, EDGES) for b in (2, 3)]
            for codes, first, count in pieces:
                for half in range(HALVES):
                    nc.tensor.matmul_mx(
                        out=bank[:, half, first % PAIR : first % PAIR + count],
                        lhsT=w4_codes[:, 2 * P * half : 2 * P * (half + 1)].bitcast(FP4X4),
                        lhsT_scale=w4_plane[:, P * half : P * (half + 1)],
                        rhs=codes.bitcast(FP8X4),
                        rhs_scale=src_plane[:, :PAIR] if pair == 0 else src_planes[first // EDGES],
                        start=True,
                        stop=True,
                    )
            return bank

        def hidden(b, y, sloped):
            y_flat = y[:].rearrange("p n t -> p (n t)")
            h = keep.tile([P, EDGES * PACK], BF16, name="h_%d" % b, align_bytes=LINE)
            if sloped is None:
                nc.vector.scalar_tensor_tensor(out=h[:], in0=y_flat, scalar=SLOPE, in1=y_flat, op0=MULT, op1=MAX)
            else:
                sloped_flat = sloped[:].rearrange("p n t -> p (n t)")
                for part in (slice(0, 2 * EDGES), slice(2 * EDGES, 4 * EDGES)):
                    nc.vector.tensor_tensor(out=h[:, part], in0=y_flat[:, part], in1=sloped_flat[:, part], op=MAX)
            return h

        def scores(b, h):
            h_codes = keep.tile([P, EDGES], U32, name="h_codes_%d" % b, align_bytes=LINE)
            h_plane = keep.tile([P, EDGES], U8, name="h_plane_%d" % b, align_bytes=LINE)
            parts = 1 if b < BLOCKS - 1 else 2
            for part in range(parts):
                c0, c1 = part * EDGES // parts, (part + 1) * EDGES // parts
                nc.vector.quantize_mx(out=h_codes[:, c0:c1].bitcast(FP8X4), scales=h_plane[:, c0:c1], in_=h[:, PACK * c0 : PACK * c1])
            score_bank = psum.tile([P, HALVES, EDGES], F32, name="score_bank_%d" % b)
            sums = [score_bank[:, half, :] for half in range(HALVES)]
            if b == BLOCKS - 1:
                sums[1] = psum.tile([P, EDGES], F32, name="last_scores", tag="y_bank_2")[:]
            for half in range(HALVES):
                nc.tensor.matmul_mx(
                    out=sums[half],
                    lhsT=w3_codes[:, 2 * P * half : 2 * P * (half + 1)].bitcast(FP4X4),
                    lhsT_scale=w3_plane[:, P * half : P * (half + 1)],
                    rhs=h_codes[:].bitcast(FP8X4),
                    rhs_scale=h_plane[:],
                    start=True,
                    stop=True,
                )
            e = keep.tile([P, HALVES, EDGES], F32, name="e_%d" % b, align_bytes=LINE)
            if b < BLOCKS - 1:
                nc.scalar.activation(out=e[:], in_=score_bank[:], func=SIGMOID)
            else:
                for half in range(HALVES):
                    nc.scalar.activation(out=e[:, half, :], in_=sums[half], func=SIGMOID)
            return e

        ys = [first_layer(b) for b in range(BLOCKS)]
        messages = [message_pair(pair) for pair in range(BLOCKS // 2)]
        hs = [hidden(0, *ys[0])]
        es = []
        for b in range(BLOCKS):
            if b + 1 < BLOCKS:
                hs.append(hidden(b + 1, *ys[b + 1]))
            es.append(scores(b, hs[b]))
        results = [keep.tile([P, HALVES, PAIR], F32, name="result_%d" % pair, align_bytes=LINE) for pair in range(BLOCKS // 2)]
        out_view = out.rearrange("(half p) n -> p half n", p=P)

        for b in range(BLOCKS):
            pair = b // 2
            within = slice((b % 2) * EDGES, (b % 2 + 1) * EDGES)
            if b < BLOCKS - 1:
                nc.vector.tensor_tensor(out=results[pair][:, :, within], in0=messages[pair][:, :, within], in1=es[b][:], op=MULT)
            else:
                for half in range(HALVES):
                    nc.vector.tensor_tensor(out=results[pair][:, half, within], in0=messages[pair][:, half, within], in1=es[b][:, half, :], op=MULT)
                    nc.sync.dma_start(out=out_view[:, half, PAIR:], in_=results[pair][:, half, :])
            if b == 1:
                nc.sync.dma_start(out=out_view[:, :, :PAIR], in_=results[pair][:])
